import numpy as np
import ml_dtypes


def mxq(x, axis, fmt="e4m3"):
    dtype, down = {"e4m3": (ml_dtypes.float8_e4m3fn, 7), "e5m2": (ml_dtypes.float8_e5m2, 14)}[fmt]
    v = np.moveaxis(np.asarray(x, np.float32).astype(ml_dtypes.bfloat16).astype(np.float64), axis, -1)
    blocks = v.reshape(v.shape[:-1] + (-1, 32))
    amax = np.abs(blocks).max(-1, keepdims=True)
    byte = np.maximum(np.where(amax > 0, np.frexp(amax)[1] - 1 + 127, 0) - down, 1)
    scale = np.exp2(byte - 127.0)
    codes = (blocks / scale).astype(np.float32).astype(dtype).astype(np.float64)
    return np.moveaxis((codes * scale).reshape(v.shape), -1, axis)


WIDE = False


def mx_kscale(k):
    if not WIDE:
        return np.ones(k)
    levels = np.array([10, -10, 5, -5, 0])
    if k % 512:
        return np.exp2(np.random.permutation(np.resize(levels, k // 32))).repeat(32)
    a = np.empty((k // 512, 16))
    for p in range(k // 512):
        a[p, :8] = np.random.permutation(np.resize(levels, 8))
        for g in range(8):
            far = levels[np.abs(levels - a[p, g]) >= 10]
            a[p, g + 8] = far[np.random.randint(len(far))]
    return np.exp2(a.ravel()).repeat(32)


def f64(x):
    return np.asarray(x).astype(np.float64)


def striped(idx):
    return np.tile(idx.reshape(-1, 16).T, (8, 1)).astype(np.uint16)


def unstriped(offs):
    return offs[:16].T.reshape(-1).astype(np.int64)


E2M1 = np.array([0.0, 0.5, 1.0, 1.5, 2.0, 3.0, 4.0, 6.0, -0.0, -0.5, -1.0, -1.5, -2.0, -3.0, -4.0, -6.0])


def pack_weight(w, fmt):
    k, n = w.shape
    w = f64(np.asarray(w, np.float32).astype(ml_dtypes.bfloat16)).reshape(k // 32, 32, n)
    amax = np.abs(w).max(1)
    if fmt == "e4m3":
        byte = np.frexp(amax)[1] - 1 + 127 - 7
    else:
        mant, ex = np.frexp(amax / 6.0)
        byte = np.where(mant > 0.5, ex, ex - 1) + 127
    byte = np.clip(np.where(amax > 0, byte, 1), 1, 254)
    scaled = (w * np.exp2(127.0 - byte)[:, None, :]).reshape(k, n).astype(np.float32)
    by_word = np.ascontiguousarray(scaled.reshape(k // 512, 128, 4, n).transpose(0, 1, 3, 2))
    if fmt == "e4m3":
        words = by_word.astype(ml_dtypes.float8_e4m3fn).view(np.uint8)
    else:
        c = by_word.astype(ml_dtypes.float4_e2m1fn).view(np.uint8) & 0xF
        words = (c[..., 0::2] | (c[..., 1::2] << 4)).reshape(k // 512, 128, 2 * n)
    return np.ascontiguousarray(words), np.ascontiguousarray(byte.astype(np.uint8).reshape(k // 512, 16, n))


def unpack_weight(words, scales, fmt):
    g, _, n = scales.shape
    words = np.ascontiguousarray(words).reshape(g, 128, n, -1)
    if fmt == "e4m3":
        vals = words.view(ml_dtypes.float8_e4m3fn).astype(np.float64)
    else:
        nib = np.empty((g, 128, n, 4), np.uint8)
        nib[..., 0::2] = words & 0xF
        nib[..., 1::2] = words >> 4
        vals = E2M1[nib]
    vals = vals * np.repeat(np.exp2(scales.astype(np.float64) - 127.0), 8, axis=1)[..., None]
    return vals.transpose(0, 1, 3, 2).reshape(g * 512, n)


def gelu(v):
    return 0.5 * v * (1.0 + np.tanh(np.sqrt(2.0 / np.pi) * (v + 0.044715 * v**3)))


K, T, S, P, H, N = 1536, 4096, 1024, 512, 1024, 768

def setup_inputs():
    n = np.random.standard_normal
    s = mx_kscale(K)[:, None]
    u = mx_kscale(H)[:, None]
    tab_words, tab_scales = pack_weight(n((K, T)) * s, "e4m3")
    w2_words, w2_scales = pack_weight(n((H, N)) / np.sqrt(H) / u, "e2m1")
    return {
        "tab_words": tab_words, "tab_scales": tab_scales,
        "offs": striped(np.random.permutation(T)[:S]),
        "pos1": striped(np.random.permutation(S)[:P]),
        "pos2": striped(np.random.permutation(S)[:P]),
        "w1": (n((K, H)) / np.sqrt(K) / s).astype(np.float32),
        "bg": (0.5 * n(H)).astype(np.float32),
        "gain": (np.exp(0.3 * n(H)) * u[:, 0]).astype(np.float32),
        "w2_words": w2_words, "w2_scales": w2_scales,
    }

def reference(tab_words, tab_scales, offs, pos1, pos2, w1, bg, gain, w2_words, w2_scales):
    v = unpack_weight(tab_words, tab_scales, "e4m3")[:, unstriped(offs)]
    w1q = mxq(f64(w1), 0, "e4m3")
    h = w1q.T @ v
    a = h[:, unstriped(pos1)]
    b = h[:, unstriped(pos2)]
    gate = 1.0 / (1.0 + np.exp(-(a + f64(bg)[:, None])))
    z = gate * b * f64(gain)[:, None]
    zq = mxq(z, 0, "e4m3")
    w2 = unpack_weight(w2_words, w2_scales, "e2m1")
    return w2.T @ zq

@@ -1,0 +1,276 @@
+from contextlib import ExitStack
+
+import concourse.mybir as mybir
+
+K, T, S, E, H, N = 1536, 4096, 1024, 512, 1024, 768
+FLOPS = 2 * K * H * S + 2 * H * N * E
+
+F32 = mybir.dt.float32
+BF16 = mybir.dt.bfloat16
+I32 = mybir.dt.int32
+U32 = mybir.dt.uint32
+U16 = mybir.dt.uint16
+U8 = mybir.dt.uint8
+FP8X4 = mybir.dt.float8_e4m3fn_x4
+FP4X4 = mybir.dt.float4_e2m1fn_x4
+MULT = mybir.AluOpType.mult
+COPY = mybir.ActivationFunctionType.Copy
+SIGMOID = mybir.ActivationFunctionType.Sigmoid
+
+P = 128
+PACK = 4
+K_PASS = P * PACK
+BANK = 512
+PASSES1 = K // K_PASS
+PASSES2 = H // K_PASS
+N_TILES = N // P
+EDGE_PARTS = ((0, 256), (256, 128), (384, 128))
+SPLIT_M = 88
+
+
+def tile_list_gated_edge_messages_kernel(
+    tc, tab_words, tab_scales, offs, pos1, pos2, w1, bg, gain, w2_words, w2_scales, out
+):
+    nc = tc.nc
+    with ExitStack() as ctx:
+        keep = ctx.enter_context(tc.tile_pool(name="keep", bufs=1))
+        raw_pool = ctx.enter_context(tc.tile_pool(name="raw", bufs=4))
+        cast_pool = ctx.enter_context(tc.tile_pool(name="cast", bufs=3))
+        gate_pool = ctx.enter_context(tc.tile_pool(name="gate", bufs=6))
+        psum = ctx.enter_context(tc.psum_pool(name="psum", bufs=1))
+
+        offs_sb = keep.tile([P, S // 16], U16, name="offs_sb")
+        pos1_sb = keep.tile([P, E // 16], U16, name="pos1_sb")
+        pos2_sb = keep.tile([P, E // 16], U16, name="pos2_sb")
+        tab_sc = keep.tile([P, T], U8, name="tab_sc", align_bytes=64)
+        w2_sc = keep.tile([P, PASSES2, N], U8, name="w2_sc", align_bytes=64)
+        w2_sb = keep.tile([P, PASSES2, 2 * N], U8, name="w2_sb", align_bytes=64)
+        bg_sb = keep.tile([P, PASSES2, PACK], F32, name="bg_sb")
+        gain_sb = keep.tile([P, PASSES2, PACK], F32, name="gain_sb")
+        warm = keep.tile([P, PACK], F32, name="warm")
+        tab_sb = [keep.tile([P, T], I32, name=f"tab{a}", align_bytes=64) for a in range(PASSES1)]
+        v_codes = [keep.tile([P, S], U32, name=f"v_codes{a}", align_bytes=64) for a in range(PASSES1)]
+        v_sc = keep.tile([P, S], U8, name="v_sc", align_bytes=64)
+        h_sb = [[keep.tile([P, S], F32, name=f"h{b}_{t}") for t in range(PACK)] for b in range(PASSES2)]
+
+        nc.vector.memset(tab_sc[:].bitcast(I32), 0)
+        nc.vector.memset(w2_sc[:].rearrange("p a n -> p (a n)").bitcast(I32), 0)
+
+        nc.gpsimd.memset(warm[:], 0.0)
+        nc.scalar.activation(warm[:], warm[:], SIGMOID)
+
+        raw = {}
+
+        def load_table(a):
+            nc.sync.dma_start(out=tab_sb[a][:], in_=tab_words[a].rearrange("p t i -> p (t i)").bitcast(I32))
+
+        def load_w1(b, a):
+            raw[b, a] = raw_pool.tile([P, PACK, K_PASS], F32, name="raw")
+            rows = w1[a * K_PASS : (a + 1) * K_PASS, b * K_PASS : (b + 1) * K_PASS]
+            nc.sync.dma_start(out=raw[b, a][:], in_=rows.rearrange("(p j) c -> p j c", j=PACK))
+
+        load_table(0)
+        nc.sync.dma_start(offs_sb[:], offs)
+        for q in range(4):
+            nc.sync.dma_start(
+                out=tab_sc[32 * q : 32 * q + 4 * PASSES1, :].bitcast(I32),
+                in_=tab_scales[:, 4 * q : 4 * q + 4, :].bitcast(I32),
+            )
+        load_w1(0, 0)
+        load_table(1)
+        load_w1(0, 1)
+        load_table(2)
+        load_w1(0, 2)
+        nc.sync.dma_start(pos1_sb[:], pos1)
+        nc.sync.dma_start(pos2_sb[:], pos2)
+        nc.sync.dma_start(out=bg_sb[:], in_=bg.rearrange("(b p t) -> p b t", p=P, t=PACK))
+        nc.sync.dma_start(out=gain_sb[:], in_=gain.rearrange("(b p t) -> p b t", p=P, t=PACK))
+
+        grouped, w1_codes, w1_sc = {}, {}, {}
+
+        def cast_w1(copy, b, a, pair, m0=0, m1=P):
+            if (b, a) not in grouped:
+                grouped[b, a] = cast_pool.tile([P, PACK, P, PACK], BF16, name="grouped", align_bytes=64)
+            ts = slice(2 * pair, 2 * pair + 2)
+            src = raw[b, a][:].rearrange("p j (m t) -> p m j t", t=PACK)[:, m0:m1, :, ts]
+            dst = grouped[b, a][:].rearrange("p t m j -> p m j t")[:, m0:m1, :, ts]
+            copy(dst, src)
+
+        def quantize_w1(b, a, t0=0, t1=PACK):
+            if (b, a) not in w1_codes:
+                w1_codes[b, a] = keep.tile([P, K_PASS], U32, name=f"w1_codes{b}_{a}", align_bytes=64)
+                w1_sc[b, a] = keep.tile([P, K_PASS], U8, name=f"w1_sc{b}_{a}", align_bytes=64)
+            cols = slice(t0 * P, t1 * P)
+            nc.vector.quantize_mx(
+                out=w1_codes[b, a][:, cols].bitcast(FP8X4),
+                scales=w1_sc[b, a][:, cols],
+                in_=grouped[b, a][:, t0:t1, :, :].rearrange("p t m j -> p (t m j)"),
+            )
+
+        def gather_words(a):
+            nc.vector.tensor_copy(v_codes[a][:], tab_sb[a][:].bitcast(U32).indirect(offs_sb[:]))
+
+        h_ps = {}
+
+        def project(b, t, a):
+            for half in range(2):
+                if a == 0:
+                    h_ps[b, t, half] = psum.tile([P, BANK], F32, name=f"bank{2 * t + half}")
+                cols = slice(half * BANK, (half + 1) * BANK)
+                nc.tensor.matmul_mx(
+                    out=h_ps[b, t, half][:],
+                    lhsT=w1_codes[b, a][:, t * P : (t + 1) * P].bitcast(FP8X4),
+                    lhsT_scale=w1_sc[b, a][:, t * P : (t + 1) * P],
+                    rhs=v_codes[a][:, cols].bitcast(FP8X4),
+                    rhs_scale=v_sc[4 * a :, cols],
+                    start=(a == 0),
+                    stop=(a == PASSES1 - 1),
+                )
+
+        def empty_h(b, t, copies):
+            for half in range(2):
+                copies[half](h_sb[b][t][:, half * BANK : (half + 1) * BANK], h_ps[b, t, half][:])
+
+        gate, zf, z_codes, z_sc = {}, {}, {}, {}
+
+        def receiver(b, t):
+            gate[b, t] = gate_pool.tile([P, E], F32, name="gate")
+            nc.vector.tensor_copy(gate[b, t][:], h_sb[b][t][:].indirect(pos1_sb[:]))
+            nc.scalar.activation(gate[b, t][:], gate[b, t][:], SIGMOID, bias=bg_sb[:, b, t : t + 1])
+            if b == 1:
+                nc.scalar.activation(gate[b, t][:], gate[b, t][:], COPY, scale=gain_sb[:, b, t : t + 1])
+
+        def sender(b, t, j0, n):
+            if (b, j0) not in zf:
+                zf[b, j0] = keep.tile([P, PACK, n], F32, name=f"zf{b}_{j0}")
+            nc.vector.tensor_tensor(
+                zf[b, j0][:, t, :],
+                h_sb[b][t][:].indirect(pos2_sb[:, j0 // 16 : (j0 + n) // 16]),
+                gate[b, t][:, j0 : j0 + n],
+                MULT,
+            )
+
+        zb = {}
+
+        def scale_z(c0, c1):
+            if (0, 0) not in zb:
+                zb[0, 0] = keep.tile([P, E * PACK], BF16, name="zb0_0", align_bytes=64)
+            nc.vector.tensor_tensor(
+                zb[0, 0][:].rearrange("p (c i t) -> p c t i", i=4, t=PACK)[:, c0:c1],
+                zf[0, 0][:].rearrange("p t (c i) -> p c t i", i=4)[:, c0:c1],
+                gain_sb[:, 0, :].unsqueeze(1).unsqueeze(3).to_broadcast([P, c1 - c0, PACK, 4]),
+                MULT,
+            )
+
+        def round_z(j0, n):
+            zb[1, j0] = keep.tile([P, n * PACK], BF16, name=f"zb1_{j0}", align_bytes=64)
+            nc.vector.tensor_copy(
+                zb[1, j0][:].rearrange("p (c i t) -> p c t i", i=4, t=PACK),
+                zf[1, j0][:].rearrange("p t (c i) -> p c t i", i=4),
+            )
+
+        def quantize_z(b, j0, n):
+            z_codes[b, j0] = keep.tile([P, n], U32, name=f"z_codes{b}_{j0}", align_bytes=64)
+            z_sc[b, j0] = keep.tile([P, n], U8, name=f"z_sc{b}_{j0}", align_bytes=64)
+            nc.vector.quantize_mx(out=z_codes[b, j0][:].bitcast(FP8X4), scales=z_sc[b, j0][:], in_=zb[b, j0][:])
+
+        def messages(j0, n, first_bank, tiles_per_bank, copies):
+            for g in range(N_TILES // tiles_per_bank):
+                acc = psum.tile([P, tiles_per_bank, n], F32, name=f"bank{first_bank + g}")
+                for u in range(tiles_per_bank):
+                    nt = g * tiles_per_bank + u
+                    for c0 in range(0, n, P):
+                        for b in range(PASSES2):
+                            key, z0 = ((0, 0), j0 + c0) if b == 0 else ((1, j0), c0)
+                            nc.tensor.matmul_mx(
+                                out=acc[:, u, c0 : c0 + P],
+                                lhsT=w2_sb[:, b, 2 * P * nt : 2 * P * (nt + 1)].bitcast(FP4X4),
+                                lhsT_scale=w2_sc[:, b, P * nt : P * (nt + 1)],
+                                rhs=z_codes[key][:, z0 : z0 + P].bitcast(FP8X4),
+                                rhs_scale=z_sc[key][:, z0 : z0 + P],
+                                start=(b == 0),
+                                stop=(b == PASSES2 - 1),
+                            )
+                res = keep.tile([P, tiles_per_bank, n], F32, name=f"res{j0}_{g}")
+                copies[g](res[:], acc[:])
+                rows = out[g * tiles_per_bank * P : (g + 1) * tiles_per_bank * P, j0 : j0 + n]
+                nc.sync.dma_start(out=rows.rearrange("(u p) j -> p u j", p=P), in_=res[:])
+
+        vcopy, scopy = nc.vector.tensor_copy, nc.scalar.copy
+
+        gather_words(0)
+        nc.vector.tensor_copy(v_sc[:], tab_sc[:].indirect(offs_sb[:]))
+        for a in range(PASSES1 - 1):
+            cast_w1(scopy, 0, a, 0)
+            cast_w1(scopy, 0, a, 1)
+            quantize_w1(0, a)
+            for t in range(PACK):
+                project(0, t, a)
+            gather_words(a + 1)
+        last = PASSES1 - 1
+        for a in range(PASSES1):
+            load_w1(1, a)
+        nc.sync.dma_start(out=w2_sb[:].bitcast(I32), in_=w2_words.rearrange("a p n -> p a n").bitcast(I32))
+        for q in range(4):
+            nc.sync.dma_start(
+                out=w2_sc[32 * q : 32 * q + 4, :, :].bitcast(I32),
+                in_=w2_scales[:, 4 * q : 4 * q + 4, :].rearrange("a r n -> r a n").bitcast(I32),
+            )
+        cast_w1(vcopy, 0, last, 0, 0, SPLIT_M)
+        cast_w1(scopy, 0, last, 0, SPLIT_M, P)
+        cast_w1(scopy, 0, last, 1)
+        quantize_w1(0, last, 0, 1)
+        project(0, 0, last)
+        quantize_w1(0, last, 1, 2)
+        project(0, 1, last)
+        empty_h(0, 0, (scopy, vcopy))
+        quantize_w1(0, last, 2, 4)
+        project(0, 2, last)
+        project(0, 3, last)
+
+        empty_h(0, 1, (scopy, scopy))
+        receiver(0, 0)
+        receiver(0, 1)
+        empty_h(0, 2, (scopy, scopy))
+        sender(0, 0, 0, E)
+        cast_w1(scopy, 1, 0, 0)
+        cast_w1(scopy, 1, 0, 1)
+        receiver(0, 2)
+        empty_h(0, 3, (scopy, scopy))
+        sender(0, 1, 0, E)
+        quantize_w1(1, 0)
+        receiver(0, 3)
+        cast_w1(scopy, 1, 1, 0)
+        cast_w1(scopy, 1, 1, 1)
+        sender(0, 2, 0, E)
+        quantize_w1(1, 1)
+        cast_w1(scopy, 1, 2, 0)
+        sender(0, 3, 0, E)
+        quantize_w1(1, 2, 0, 2)
+        cast_w1(scopy, 1, 2, 1)
+        for t in range(2):
+            for a in range(PASSES1):
+                project(1, t, a)
+        empty_h(1, 0, (scopy, vcopy))
+        quantize_w1(1, 2, 2, 4)
+        for t in range(2, PACK):
+            for a in range(PASSES1):
+                project(1, t, a)
+        for t in range(1, PACK):
+            empty_h(1, t, (scopy, scopy))
+        for t in range(PACK):
+            receiver(1, t)
+        for i in range(PACK):
+            scale_z(i * 32, (i + 1) * 32)
+        quantize_z(0, 0, E)
+        parts = E // P
+        for part in range(parts):
+            sender(1, 0, part * P, P)
+            if part > 0:
+                quantize_z(1, (part - 1) * P, P)
+                messages((part - 1) * P, P, 2 * (part - 1), 3, (scopy, scopy))
+            for t in range(1, PACK):
+                sender(1, t, part * P, P)
+            round_z(part * P, P)
+        quantize_z(1, (parts - 1) * P, P)
+        messages((parts - 1) * P, P, 2 * (parts - 1), 3, (scopy, vcopy))

@@ -137,8 +137,6 @@ def tile_list_gated_edge_messages_kernel(
             gate[b, t] = gate_pool.tile([P, E], F32, name="gate")
             nc.vector.tensor_copy(gate[b, t][:], h_sb[b][t][:].indirect(pos1_sb[:]))
             nc.scalar.activation(gate[b, t][:], gate[b, t][:], SIGMOID, bias=bg_sb[:, b, t : t + 1])
-            if b == 1:
-                nc.scalar.activation(gate[b, t][:], gate[b, t][:], COPY, scale=gain_sb[:, b, t : t + 1])
 
         def sender(b, t, j0, n):
             if (b, j0) not in zf:
@@ -152,49 +150,75 @@ def tile_list_gated_edge_messages_kernel(
 
         zb = {}
 
-        def scale_z(c0, c1):
-            if (0, 0) not in zb:
-                zb[0, 0] = keep.tile([P, E * PACK], BF16, name="zb0_0", align_bytes=64)
-            nc.vector.tensor_tensor(
-                zb[0, 0][:].rearrange("p (c i t) -> p c t i", i=4, t=PACK)[:, c0:c1],
-                zf[0, 0][:].rearrange("p t (c i) -> p c t i", i=4)[:, c0:c1],
-                gain_sb[:, 0, :].unsqueeze(1).unsqueeze(3).to_broadcast([P, c1 - c0, PACK, 4]),
-                MULT,
+        def z_views(b, key, j0, n):
+            if (b, key) not in zb:
+                zb[b, key] = keep.tile([P, zf[b, key].shape[2] * PACK], BF16, name=f"zb{b}_{key}", align_bytes=64)
+            cs = slice(j0 // 4, (j0 + n) // 4)
+            return (
+                zb[b, key][:].rearrange("p (c i t) -> p c t i", i=4, t=PACK)[:, cs],
+                zf[b, key][:].rearrange("p t (c i) -> p c t i", i=4)[:, cs],
             )
 
-        def round_z(j0, n):
-            zb[1, j0] = keep.tile([P, n * PACK], BF16, name=f"zb1_{j0}", align_bytes=64)
-            nc.vector.tensor_copy(
-                zb[1, j0][:].rearrange("p (c i t) -> p c t i", i=4, t=PACK),
-                zf[1, j0][:].rearrange("p t (c i) -> p c t i", i=4),
+        def finish_v(b, key, j0, n):
+            dst, src = z_views(b, key, j0, n)
+            factor = gain_sb[:, b, :].unsqueeze(1).unsqueeze(3).to_broadcast([P, n // 4, PACK, 4])
+            nc.vector.tensor_tensor(dst, src, factor, MULT)
+
+        def finish_s(b, key, j0, n):
+            for t in range(PACK):
+                piece = zf[b, key][:, t, j0 : j0 + n]
+                nc.scalar.activation(piece, piece, COPY, scale=gain_sb[:, b, t : t + 1])
+            scopy(*z_views(b, key, j0, n))
+
+        def quantize_z(b, key, j0, n):
+            if (b, key) not in z_codes:
+                width = zf[b, key].shape[2]
+                z_codes[b, key] = keep.tile([P, width], U32, name=f"z_codes{b}_{key}", align_bytes=64)
+                z_sc[b, key] = keep.tile([P, width], U8, name=f"z_sc{b}_{key}", align_bytes=64)
+            nc.vector.quantize_mx(
+                out=z_codes[b, key][:, j0 : j0 + n].bitcast(FP8X4),
+                scales=z_sc[b, key][:, j0 : j0 + n],
+                in_=zb[b, key][:, PACK * j0 : PACK * (j0 + n)],
             )
 
-        def quantize_z(b, j0, n):
-            z_codes[b, j0] = keep.tile([P, n], U32, name=f"z_codes{b}_{j0}", align_bytes=64)
-            z_sc[b, j0] = keep.tile([P, n], U8, name=f"z_sc{b}_{j0}", align_bytes=64)
-            nc.vector.quantize_mx(out=z_codes[b, j0][:].bitcast(FP8X4), scales=z_sc[b, j0][:], in_=zb[b, j0][:])
+        def message_pass(acc, nt, j0, b):
+            key, z0 = ((0, 0), j0) if b == 0 else ((1, j0), 0)
+            nc.tensor.matmul_mx(
+                out=acc,
+                lhsT=w2_sb[:, b, 2 * P * nt : 2 * P * (nt + 1)].bitcast(FP4X4),
+                lhsT_scale=w2_sc[:, b, P * nt : P * (nt + 1)],
+                rhs=z_codes[key][:, z0 : z0 + P].bitcast(FP8X4),
+                rhs_scale=z_sc[key][:, z0 : z0 + P],
+                start=(b == 0),
+                stop=(b == PASSES2 - 1),
+            )
 
-        def messages(j0, n, first_bank, tiles_per_bank, copies):
-            for g in range(N_TILES // tiles_per_bank):
-                acc = psum.tile([P, tiles_per_bank, n], F32, name=f"bank{first_bank + g}")
-                for u in range(tiles_per_bank):
-                    nt = g * tiles_per_bank + u
-                    for c0 in range(0, n, P):
-                        for b in range(PASSES2):
-                            key, z0 = ((0, 0), j0 + c0) if b == 0 else ((1, j0), c0)
-                            nc.tensor.matmul_mx(
-                                out=acc[:, u, c0 : c0 + P],
-                                lhsT=w2_sb[:, b, 2 * P * nt : 2 * P * (nt + 1)].bitcast(FP4X4),
-                                lhsT_scale=w2_sc[:, b, P * nt : P * (nt + 1)],
-                                rhs=z_codes[key][:, z0 : z0 + P].bitcast(FP8X4),
-                                rhs_scale=z_sc[key][:, z0 : z0 + P],
-                                start=(b == 0),
-                                stop=(b == PASSES2 - 1),
-                            )
-                res = keep.tile([P, tiles_per_bank, n], F32, name=f"res{j0}_{g}")
-                copies[g](res[:], acc[:])
-                rows = out[g * tiles_per_bank * P : (g + 1) * tiles_per_bank * P, j0 : j0 + n]
-                nc.sync.dma_start(out=rows.rearrange("(u p) j -> p u j", p=P), in_=res[:])
+        def store(res, g, j0):
+            rows = out[g * 3 * P : (g + 1) * 3 * P, j0 : j0 + P]
+            nc.sync.dma_start(out=rows.rearrange("(u p) j -> p u j", p=P), in_=res[:])
+
+        def messages(j0, first_bank):
+            for g in range(2):
+                acc = psum.tile([P, 3, P], F32, name=f"bank{first_bank + g}")
+                for u in range(3):
+                    for b in range(PASSES2):
+                        message_pass(acc[:, u, :], 3 * g + u, j0, b)
+                res = keep.tile([P, 3, P], F32, name=f"res{j0}_{g}")
+                scopy(res[:], acc[:])
+                store(res, g, j0)
+
+        def last_messages(j0):
+            acc = [psum.tile([P, P], F32, name=f"bank{2 + nt}") for nt in range(N_TILES)]
+            res = [keep.tile([P, 3, P], F32, name=f"res{j0}_{g}") for g in range(2)]
+            for b in range(PASSES2):
+                for u in range(3):
+                    for g in range(2):
+                        message_pass(acc[3 * g + u][:], 3 * g + u, j0, b)
+            for u in range(3):
+                scopy(res[0][:, u, :], acc[u][:])
+                vcopy(res[1][:, u, :], acc[3 + u][:])
+            for g in range(2):
+                store(res[g], g, j0)
 
         vcopy, scopy = nc.vector.tensor_copy, nc.scalar.copy
 
@@ -251,7 +275,7 @@ def tile_list_gated_edge_messages_kernel(
         for t in range(2):
             for a in range(PASSES1):
                 project(1, t, a)
-        empty_h(1, 0, (scopy, vcopy))
+        empty_h(1, 0, (scopy, scopy))
         quantize_w1(1, 2, 2, 4)
         for t in range(2, PACK):
             for a in range(PASSES1):
@@ -260,17 +284,19 @@ def tile_list_gated_edge_messages_kernel(
             empty_h(1, t, (scopy, scopy))
         for t in range(PACK):
             receiver(1, t)
-        for i in range(PACK):
-            scale_z(i * 32, (i + 1) * 32)
-        quantize_z(0, 0, E)
+        for part in range(3):
+            finish_v(0, 0, part * P, P)
+        quantize_z(0, 0, 0, 2 * P)
+        finish_s(0, 0, 3 * P, P)
         parts = E // P
         for part in range(parts):
-            sender(1, 0, part * P, P)
-            if part > 0:
-                quantize_z(1, (part - 1) * P, P)
-                messages((part - 1) * P, P, 2 * (part - 1), 3, (scopy, scopy))
-            for t in range(1, PACK):
+            for t in range(PACK):
                 sender(1, t, part * P, P)
-            round_z(part * P, P)
-        quantize_z(1, (parts - 1) * P, P)
-        messages((parts - 1) * P, P, 2 * (parts - 1), 3, (scopy, vcopy))
+            if part == 1:
+                quantize_z(0, 0, 2 * P, 2 * P)
+            (finish_s, finish_s, finish_v, finish_v)[part](1, part * P, 0, P)
+            quantize_z(1, part * P, 0, P)
+            if part == parts - 1:
+                last_messages(part * P)
+            else:
+                messages(part * P, 2 * (part % 2))

@@ -37,6 +37,7 @@ def tile_list_gated_edge_messages_kernel(
         raw_pool = ctx.enter_context(tc.tile_pool(name="raw", bufs=4))
         cast_pool = ctx.enter_context(tc.tile_pool(name="cast", bufs=3))
         gate_pool = ctx.enter_context(tc.tile_pool(name="gate", bufs=6))
+        zf_pool = ctx.enter_context(tc.tile_pool(name="zf", bufs=3))
         psum = ctx.enter_context(tc.psum_pool(name="psum", bufs=1))
 
         offs_sb = keep.tile([P, S // 16], U16, name="offs_sb")
@@ -57,6 +58,11 @@ def tile_list_gated_edge_messages_kernel(
         nc.vector.memset(w2_sc[:].rearrange("p a n -> p (a n)").bitcast(I32), 0)
 
         nc.gpsimd.memset(warm[:], 0.0)
+        for q in range(4):
+            nc.gpsimd.dma_start(
+                out=tab_sc[32 * q : 32 * q + 4 * PASSES1, :].bitcast(I32),
+                in_=tab_scales[:, 4 * q : 4 * q + 4, :].bitcast(I32),
+            )
         nc.scalar.activation(warm[:], warm[:], SIGMOID)
 
         raw = {}
@@ -71,11 +77,6 @@ def tile_list_gated_edge_messages_kernel(
 
         load_table(0)
         nc.sync.dma_start(offs_sb[:], offs)
-        for q in range(4):
-            nc.sync.dma_start(
-                out=tab_sc[32 * q : 32 * q + 4 * PASSES1, :].bitcast(I32),
-                in_=tab_scales[:, 4 * q : 4 * q + 4, :].bitcast(I32),
-            )
         load_w1(0, 0)
         load_table(1)
         load_w1(0, 1)
@@ -90,7 +91,8 @@ def tile_list_gated_edge_messages_kernel(
 
         def cast_w1(copy, b, a, pair, m0=0, m1=P):
             if (b, a) not in grouped:
-                grouped[b, a] = cast_pool.tile([P, PACK, P, PACK], BF16, name="grouped", align_bytes=64)
+                pool, tag = (keep, "shared") if (b, a) == (1, 0) else (cast_pool, "grouped")
+                grouped[b, a] = pool.tile([P, PACK, P, PACK], BF16, name=tag, align_bytes=64)
             ts = slice(2 * pair, 2 * pair + 2)
             src = raw[b, a][:].rearrange("p j (m t) -> p m j t", t=PACK)[:, m0:m1, :, ts]
             dst = grouped[b, a][:].rearrange("p t m j -> p m j t")[:, m0:m1, :, ts]
@@ -98,7 +100,8 @@ def tile_list_gated_edge_messages_kernel(
 
         def quantize_w1(b, a, t0=0, t1=PACK):
             if (b, a) not in w1_codes:
-                w1_codes[b, a] = keep.tile([P, K_PASS], U32, name=f"w1_codes{b}_{a}", align_bytes=64)
+                tag = "shared" if (b, a) == (0, PASSES1 - 1) else f"w1_codes{b}_{a}"
+                w1_codes[b, a] = keep.tile([P, K_PASS], U32, name=tag, align_bytes=64)
                 w1_sc[b, a] = keep.tile([P, K_PASS], U8, name=f"w1_sc{b}_{a}", align_bytes=64)
             cols = slice(t0 * P, t1 * P)
             nc.vector.quantize_mx(
@@ -140,7 +143,7 @@ def tile_list_gated_edge_messages_kernel(
 
         def sender(b, t, j0, n):
             if (b, j0) not in zf:
-                zf[b, j0] = keep.tile([P, PACK, n], F32, name=f"zf{b}_{j0}")
+                zf[b, j0] = (zf_pool if b else keep).tile([P, PACK, n], F32, name=f"zf{b}")
             nc.vector.tensor_tensor(
                 zf[b, j0][:, t, :],
                 h_sb[b][t][:].indirect(pos2_sb[:, j0 // 16 : (j0 + n) // 16]),
@@ -240,8 +243,7 @@ def tile_list_gated_edge_messages_kernel(
                 out=w2_sc[32 * q : 32 * q + 4, :, :].bitcast(I32),
                 in_=w2_scales[:, 4 * q : 4 * q + 4, :].rearrange("a r n -> r a n").bitcast(I32),
             )
-        cast_w1(vcopy, 0, last, 0, 0, SPLIT_M)
-        cast_w1(scopy, 0, last, 0, SPLIT_M, P)
+        cast_w1(vcopy, 0, last, 0)
         cast_w1(scopy, 0, last, 1)
         quantize_w1(0, last, 0, 1)
         project(0, 0, last)
@@ -252,36 +254,20 @@ def tile_list_gated_edge_messages_kernel(
         project(0, 2, last)
         project(0, 3, last)
 
-        empty_h(0, 1, (scopy, scopy))
-        receiver(0, 0)
-        receiver(0, 1)
-        empty_h(0, 2, (scopy, scopy))
-        sender(0, 0, 0, E)
-        cast_w1(scopy, 1, 0, 0)
-        cast_w1(scopy, 1, 0, 1)
-        receiver(0, 2)
-        empty_h(0, 3, (scopy, scopy))
-        sender(0, 1, 0, E)
-        quantize_w1(1, 0)
-        receiver(0, 3)
-        cast_w1(scopy, 1, 1, 0)
-        cast_w1(scopy, 1, 1, 1)
-        sender(0, 2, 0, E)
-        quantize_w1(1, 1)
-        cast_w1(scopy, 1, 2, 0)
-        sender(0, 3, 0, E)
-        quantize_w1(1, 2, 0, 2)
-        cast_w1(scopy, 1, 2, 1)
-        for t in range(2):
-            for a in range(PASSES1):
-                project(1, t, a)
-        empty_h(1, 0, (scopy, scopy))
-        quantize_w1(1, 2, 2, 4)
-        for t in range(2, PACK):
-            for a in range(PASSES1):
-                project(1, t, a)
         for t in range(1, PACK):
-            empty_h(1, t, (scopy, scopy))
+            empty_h(0, t, (scopy, scopy))
+            receiver(0, t - 1)
+        receiver(0, PACK - 1)
+        for pair in range(2):
+            for a in range(PASSES1):
+                cast_w1(scopy, 1, a, pair)
+                quantize_w1(1, a, 2 * pair, 2 * pair + 2)
+            for t in range(2 * pair, 2 * pair + 2):
+                for a in range(PASSES1):
+                    project(1, t, a)
+                empty_h(1, t, (scopy, scopy if t == 0 else scopy))
+        for t in range(PACK):
+            sender(0, t, 0, E)
         for t in range(PACK):
             receiver(1, t)
         for part in range(3):

@@ -21,67 +21,80 @@ P = 128
 PACK = 4
 K_PASS = P * PACK
 BANK = 512
-PASSES1 = K // K_PASS
-PASSES2 = H // K_PASS
-N_TILES = N // P
-EDGE_PARTS = ((0, 256), (256, 128), (384, 128))
-SPLIT_M = 88
+QUADRANTS = 4
+LIST_COLUMN = 16
+PASSES = K // K_PASS
+LAST = PASSES - 1
+HALVES = H // K_PASS
+PART = 128
+GROUP = 3
+GROUPS = N // P // GROUP
+RUN = 4
 
 
 def tile_list_gated_edge_messages_kernel(
     tc, tab_words, tab_scales, offs, pos1, pos2, w1, bg, gain, w2_words, w2_scales, out
 ):
     nc = tc.nc
+    vcopy, scopy = nc.vector.tensor_copy, nc.scalar.copy
     with ExitStack() as ctx:
         keep = ctx.enter_context(tc.tile_pool(name="keep", bufs=1))
-        raw_pool = ctx.enter_context(tc.tile_pool(name="raw", bufs=4))
+        raw_pool = ctx.enter_context(tc.tile_pool(name="raw", bufs=LAST))
         cast_pool = ctx.enter_context(tc.tile_pool(name="cast", bufs=3))
         gate_pool = ctx.enter_context(tc.tile_pool(name="gate", bufs=6))
-        zf_pool = ctx.enter_context(tc.tile_pool(name="zf", bufs=3))
         psum = ctx.enter_context(tc.psum_pool(name="psum", bufs=1))
 
-        offs_sb = keep.tile([P, S // 16], U16, name="offs_sb")
-        pos1_sb = keep.tile([P, E // 16], U16, name="pos1_sb")
-        pos2_sb = keep.tile([P, E // 16], U16, name="pos2_sb")
+        offs_sb = keep.tile([P, S // LIST_COLUMN], U16, name="offs_sb")
+        pos1_sb = keep.tile([P, E // LIST_COLUMN], U16, name="pos1_sb")
+        pos2_sb = keep.tile([P, E // LIST_COLUMN], U16, name="pos2_sb")
         tab_sc = keep.tile([P, T], U8, name="tab_sc", align_bytes=64)
-        w2_sc = keep.tile([P, PASSES2, N], U8, name="w2_sc", align_bytes=64)
-        w2_sb = keep.tile([P, PASSES2, 2 * N], U8, name="w2_sb", align_bytes=64)
-        bg_sb = keep.tile([P, PASSES2, PACK], F32, name="bg_sb")
-        gain_sb = keep.tile([P, PASSES2, PACK], F32, name="gain_sb")
+        w2_sc = keep.tile([P, HALVES, N], U8, name="w2_sc", align_bytes=64)
+        w2_sb = keep.tile([P, HALVES, 2 * N], U8, name="w2_sb", align_bytes=64)
+        bg_sb = keep.tile([P, HALVES, PACK], F32, name="bg_sb")
+        gain_sb = keep.tile([P, HALVES, PACK], F32, name="gain_sb")
         warm = keep.tile([P, PACK], F32, name="warm")
-        tab_sb = [keep.tile([P, T], I32, name=f"tab{a}", align_bytes=64) for a in range(PASSES1)]
-        v_codes = [keep.tile([P, S], U32, name=f"v_codes{a}", align_bytes=64) for a in range(PASSES1)]
+        tab_sb = [keep.tile([P, T], I32, name=f"tab{a}", align_bytes=64) for a in range(PASSES)]
+        v_codes = [keep.tile([P, S], U32, name=f"v_codes{a}", align_bytes=64) for a in range(PASSES)]
         v_sc = keep.tile([P, S], U8, name="v_sc", align_bytes=64)
-        h_sb = [[keep.tile([P, S], F32, name=f"h{b}_{t}") for t in range(PACK)] for b in range(PASSES2)]
+        h_sb = [[keep.tile([P, S], F32, name=f"h{b}_{t}") for t in range(PACK)] for b in range(HALVES)]
 
         nc.vector.memset(tab_sc[:].bitcast(I32), 0)
-        nc.vector.memset(w2_sc[:].rearrange("p a n -> p (a n)").bitcast(I32), 0)
+        nc.vector.memset(w2_sc[:].rearrange("p b n -> p (b n)").bitcast(I32), 0)
 
-        nc.gpsimd.memset(warm[:], 0.0)
-        for q in range(4):
+        nc.vector.memset(warm[:], 0.0)
+        nc.scalar.activation(warm[:], warm[:], SIGMOID)
+
+        for q in range(QUADRANTS):
             nc.gpsimd.dma_start(
-                out=tab_sc[32 * q : 32 * q + 4 * PASSES1, :].bitcast(I32),
+                out=tab_sc[32 * q : 32 * q + 4 * PASSES, :].bitcast(I32),
                 in_=tab_scales[:, 4 * q : 4 * q + 4, :].bitcast(I32),
             )
-        nc.scalar.activation(warm[:], warm[:], SIGMOID)
 
         raw = {}
 
         def load_table(a):
             nc.sync.dma_start(out=tab_sb[a][:], in_=tab_words[a].rearrange("p t i -> p (t i)").bitcast(I32))
 
-        def load_w1(b, a):
-            raw[b, a] = raw_pool.tile([P, PACK, K_PASS], F32, name="raw")
+        def load_w1_rows(a):
+            whole = raw_pool.tile([P, PACK, H], F32, name="raw")
+            rows = w1[a * K_PASS : (a + 1) * K_PASS, :]
+            nc.sync.dma_start(out=whole[:], in_=rows.rearrange("(p j) c -> p j c", j=PACK))
+            for b in range(HALVES):
+                raw[b, a] = whole[:, :, b * K_PASS : (b + 1) * K_PASS]
+
+        def load_w1_half(b, a):
+            piece = keep.tile([P, PACK, K_PASS], F32, name=f"raw{b}")
             rows = w1[a * K_PASS : (a + 1) * K_PASS, b * K_PASS : (b + 1) * K_PASS]
-            nc.sync.dma_start(out=raw[b, a][:], in_=rows.rearrange("(p j) c -> p j c", j=PACK))
+            nc.sync.dma_start(out=piece[:], in_=rows.rearrange("(p j) c -> p j c", j=PACK))
+            raw[b, a] = piece[:]
 
         load_table(0)
         nc.sync.dma_start(offs_sb[:], offs)
-        load_w1(0, 0)
+        load_w1_rows(0)
         load_table(1)
-        load_w1(0, 1)
-        load_table(2)
-        load_w1(0, 2)
+        load_w1_rows(1)
+        load_table(LAST)
+        load_w1_half(0, LAST)
         nc.sync.dma_start(pos1_sb[:], pos1)
         nc.sync.dma_start(pos2_sb[:], pos2)
         nc.sync.dma_start(out=bg_sb[:], in_=bg.rearrange("(b p t) -> p b t", p=P, t=PACK))
@@ -89,18 +102,18 @@ def tile_list_gated_edge_messages_kernel(
 
         grouped, w1_codes, w1_sc = {}, {}, {}
 
-        def cast_w1(copy, b, a, pair, m0=0, m1=P):
+        def round_w1(copy, b, a, pair):
             if (b, a) not in grouped:
-                pool, tag = (keep, "shared") if (b, a) == (1, 0) else (cast_pool, "grouped")
+                pool, tag = (keep, "shared") if (b, a) == (1, LAST) else (cast_pool, "grouped")
                 grouped[b, a] = pool.tile([P, PACK, P, PACK], BF16, name=tag, align_bytes=64)
             ts = slice(2 * pair, 2 * pair + 2)
-            src = raw[b, a][:].rearrange("p j (m t) -> p m j t", t=PACK)[:, m0:m1, :, ts]
-            dst = grouped[b, a][:].rearrange("p t m j -> p m j t")[:, m0:m1, :, ts]
+            src = raw[b, a].rearrange("p j (m t) -> p m j t", t=PACK)[:, :, :, ts]
+            dst = grouped[b, a][:].rearrange("p t m j -> p m j t")[:, :, :, ts]
             copy(dst, src)
 
         def quantize_w1(b, a, t0=0, t1=PACK):
             if (b, a) not in w1_codes:
-                tag = "shared" if (b, a) == (0, PASSES1 - 1) else f"w1_codes{b}_{a}"
+                tag = "shared" if (b, a) == (0, LAST) else f"w1_codes{b}_{a}"
                 w1_codes[b, a] = keep.tile([P, K_PASS], U32, name=tag, align_bytes=64)
                 w1_sc[b, a] = keep.tile([P, K_PASS], U8, name=f"w1_sc{b}_{a}", align_bytes=64)
             cols = slice(t0 * P, t1 * P)
@@ -116,173 +129,208 @@ def tile_list_gated_edge_messages_kernel(
         h_ps = {}
 
         def project(b, t, a):
-            for half in range(2):
+            for side in range(2):
                 if a == 0:
-                    h_ps[b, t, half] = psum.tile([P, BANK], F32, name=f"bank{2 * t + half}")
-                cols = slice(half * BANK, (half + 1) * BANK)
+                    h_ps[b, t, side] = psum.tile([P, BANK], F32, name=f"bank{2 * t + side}")
+                cols = slice(side * BANK, (side + 1) * BANK)
                 nc.tensor.matmul_mx(
-                    out=h_ps[b, t, half][:],
+                    out=h_ps[b, t, side][:],
                     lhsT=w1_codes[b, a][:, t * P : (t + 1) * P].bitcast(FP8X4),
                     lhsT_scale=w1_sc[b, a][:, t * P : (t + 1) * P],
                     rhs=v_codes[a][:, cols].bitcast(FP8X4),
                     rhs_scale=v_sc[4 * a :, cols],
                     start=(a == 0),
-                    stop=(a == PASSES1 - 1),
+                    stop=(a == LAST),
                 )
 
         def empty_h(b, t, copies):
-            for half in range(2):
-                copies[half](h_sb[b][t][:, half * BANK : (half + 1) * BANK], h_ps[b, t, half][:])
+            for side in range(2):
+                copies[side](h_sb[b][t][:, side * BANK : (side + 1) * BANK], h_ps[b, t, side][:])
 
-        gate, zf, z_codes, z_sc = {}, {}, {}, {}
+        gate, gated, woven, z_codes, z_sc = {}, {}, {}, {}, {}
 
-        def receiver(b, t):
+        def receivers(b, t):
             gate[b, t] = gate_pool.tile([P, E], F32, name="gate")
             nc.vector.tensor_copy(gate[b, t][:], h_sb[b][t][:].indirect(pos1_sb[:]))
+
+        def sigmoid(b, t):
             nc.scalar.activation(gate[b, t][:], gate[b, t][:], SIGMOID, bias=bg_sb[:, b, t : t + 1])
 
-        def sender(b, t, j0, n):
-            if (b, j0) not in zf:
-                zf[b, j0] = (zf_pool if b else keep).tile([P, PACK, n], F32, name=f"zf{b}")
+        def woven_tag(b, j0):
+            return f"woven{b}_{j0}"
+
+        held_behind = {(1, 2 * PART): woven_tag(0, 0), (1, 3 * PART): woven_tag(0, 2 * PART)}
+
+        def senders(b, t, j0, n):
+            if (b, j0) not in gated:
+                tag = held_behind.get((b, j0), f"gated{b}_{j0}")
+                gated[b, j0] = keep.tile([P, PACK, n], F32, name=tag, align_bytes=64)
             nc.vector.tensor_tensor(
-                zf[b, j0][:, t, :],
-                h_sb[b][t][:].indirect(pos2_sb[:, j0 // 16 : (j0 + n) // 16]),
+                gated[b, j0][:, t, :],
+                h_sb[b][t][:].indirect(pos2_sb[:, j0 // LIST_COLUMN : (j0 + n) // LIST_COLUMN]),
                 gate[b, t][:, j0 : j0 + n],
                 MULT,
             )
 
-        zb = {}
+        scaled = keep.tile([P, PACK, E], BF16, name="scaled", align_bytes=64)
 
-        def z_views(b, key, j0, n):
-            if (b, key) not in zb:
-                zb[b, key] = keep.tile([P, zf[b, key].shape[2] * PACK], BF16, name=f"zb{b}_{key}", align_bytes=64)
-            cs = slice(j0 // 4, (j0 + n) // 4)
+        def weave_views(b, j0, tiles):
+            woven[b, j0] = keep.tile([P, PART * PACK], BF16, name=woven_tag(b, j0), align_bytes=64)
             return (
-                zb[b, key][:].rearrange("p (c i t) -> p c t i", i=4, t=PACK)[:, cs],
-                zf[b, key][:].rearrange("p t (c i) -> p c t i", i=4)[:, cs],
+                woven[b, j0][:].rearrange("p (c i t) -> p c t i", i=RUN, t=PACK),
+                tiles.rearrange("p t (c i) -> p c t i", i=RUN),
             )
 
-        def finish_v(b, key, j0, n):
-            dst, src = z_views(b, key, j0, n)
-            factor = gain_sb[:, b, :].unsqueeze(1).unsqueeze(3).to_broadcast([P, n // 4, PACK, 4])
+        def finish_on_vector(j0):
+            dst, src = weave_views(1, j0, gated[1, j0][:])
+            factor = gain_sb[:, 1, :].unsqueeze(1).unsqueeze(3).to_broadcast([P, PART // RUN, PACK, RUN])
             nc.vector.tensor_tensor(dst, src, factor, MULT)
 
-        def finish_s(b, key, j0, n):
+        def finish_on_scalar(j0):
+            tiles = keep.tile([P, PACK, PART], BF16, name=f"scaled{j0}", align_bytes=64)
             for t in range(PACK):
-                piece = zf[b, key][:, t, j0 : j0 + n]
-                nc.scalar.activation(piece, piece, COPY, scale=gain_sb[:, b, t : t + 1])
-            scopy(*z_views(b, key, j0, n))
+                nc.scalar.activation(tiles[:, t, :], gated[1, j0][:, t, :], COPY, scale=gain_sb[:, 1, t : t + 1])
+            scopy(*weave_views(1, j0, tiles[:]))
 
-        def quantize_z(b, key, j0, n):
-            if (b, key) not in z_codes:
-                width = zf[b, key].shape[2]
-                z_codes[b, key] = keep.tile([P, width], U32, name=f"z_codes{b}_{key}", align_bytes=64)
-                z_sc[b, key] = keep.tile([P, width], U8, name=f"z_sc{b}_{key}", align_bytes=64)
-            nc.vector.quantize_mx(
-                out=z_codes[b, key][:, j0 : j0 + n].bitcast(FP8X4),
-                scales=z_sc[b, key][:, j0 : j0 + n],
-                in_=zb[b, key][:, PACK * j0 : PACK * (j0 + n)],
-            )
+        def scale_first_half(t):
+            nc.scalar.activation(scaled[:, t, :], gated[0, 0][:, t, :], COPY, scale=gain_sb[:, 0, t : t + 1])
+
+        def quantize_z(b, j0):
+            z_codes[b, j0] = keep.tile([P, PART], U32, name=f"z_codes{b}_{j0}", align_bytes=64)
+            z_sc[b, j0] = keep.tile([P, PART], U8, name=f"z_sc{b}_{j0}", align_bytes=64)
+            nc.vector.quantize_mx(out=z_codes[b, j0][:].bitcast(FP8X4), scales=z_sc[b, j0][:], in_=woven[b, j0][:])
 
         def message_pass(acc, nt, j0, b):
-            key, z0 = ((0, 0), j0) if b == 0 else ((1, j0), 0)
             nc.tensor.matmul_mx(
                 out=acc,
                 lhsT=w2_sb[:, b, 2 * P * nt : 2 * P * (nt + 1)].bitcast(FP4X4),
                 lhsT_scale=w2_sc[:, b, P * nt : P * (nt + 1)],
-                rhs=z_codes[key][:, z0 : z0 + P].bitcast(FP8X4),
-                rhs_scale=z_sc[key][:, z0 : z0 + P],
+                rhs=z_codes[b, j0][:].bitcast(FP8X4),
+                rhs_scale=z_sc[b, j0][:],
                 start=(b == 0),
-                stop=(b == PASSES2 - 1),
+                stop=(b == HALVES - 1),
             )
 
-        def store(res, g, j0):
-            rows = out[g * 3 * P : (g + 1) * 3 * P, j0 : j0 + P]
+        def store(res, nt, j0):
+            rows = out[nt * P : (nt + res.shape[1]) * P, j0 : j0 + PART]
             nc.sync.dma_start(out=rows.rearrange("(u p) j -> p u j", p=P), in_=res[:])
 
         def messages(j0, first_bank):
-            for g in range(2):
-                acc = psum.tile([P, 3, P], F32, name=f"bank{first_bank + g}")
-                for u in range(3):
-                    for b in range(PASSES2):
-                        message_pass(acc[:, u, :], 3 * g + u, j0, b)
-                res = keep.tile([P, 3, P], F32, name=f"res{j0}_{g}")
+            for g in range(GROUPS):
+                acc = psum.tile([P, GROUP, PART], F32, name=f"bank{first_bank + g}")
+                for u in range(GROUP):
+                    for b in range(HALVES):
+                        message_pass(acc[:, u, :], GROUP * g + u, j0, b)
+                res = keep.tile([P, GROUP, PART], F32, name=f"res{j0}_{g}")
                 scopy(res[:], acc[:])
-                store(res, g, j0)
+                store(res, GROUP * g, j0)
 
         def last_messages(j0):
-            acc = [psum.tile([P, P], F32, name=f"bank{2 + nt}") for nt in range(N_TILES)]
-            res = [keep.tile([P, 3, P], F32, name=f"res{j0}_{g}") for g in range(2)]
-            for b in range(PASSES2):
-                for u in range(3):
-                    for g in range(2):
-                        message_pass(acc[3 * g + u][:], 3 * g + u, j0, b)
-            for u in range(3):
-                scopy(res[0][:, u, :], acc[u][:])
-                vcopy(res[1][:, u, :], acc[3 + u][:])
-            for g in range(2):
-                store(res[g], g, j0)
-
-        vcopy, scopy = nc.vector.tensor_copy, nc.scalar.copy
+            acc = [psum.tile([P, PART], F32, name=f"bank{GROUPS + nt}") for nt in range(N // P)]
+            res = [keep.tile([P, 1, PART], F32, name=f"res{j0}_{nt}") for nt in range(N // P)]
+            for b in range(HALVES):
+                for u in range(GROUP):
+                    for g in range(GROUPS):
+                        message_pass(acc[GROUP * g + u][:], GROUP * g + u, j0, b)
+            for u in range(GROUP):
+                scopy(res[u][:, 0, :], acc[u][:])
+                vcopy(res[GROUP + u][:, 0, :], acc[GROUP + u][:])
+                store(res[u], u, j0)
+                store(res[GROUP + u], GROUP + u, j0)
 
         gather_words(0)
         nc.vector.tensor_copy(v_sc[:], tab_sc[:].indirect(offs_sb[:]))
-        for a in range(PASSES1 - 1):
-            cast_w1(scopy, 0, a, 0)
-            cast_w1(scopy, 0, a, 1)
+        for a in range(LAST):
+            round_w1(scopy, 0, a, 0)
+            round_w1(scopy, 0, a, 1)
             quantize_w1(0, a)
             for t in range(PACK):
                 project(0, t, a)
             gather_words(a + 1)
-        last = PASSES1 - 1
-        for a in range(PASSES1):
-            load_w1(1, a)
-        nc.sync.dma_start(out=w2_sb[:].bitcast(I32), in_=w2_words.rearrange("a p n -> p a n").bitcast(I32))
-        for q in range(4):
+            round_w1(scopy, 1, a, 0)
+            round_w1(vcopy if a == LAST - 1 else scopy, 1, a, 1)
+            quantize_w1(1, a)
+        load_w1_half(1, LAST)
+        nc.sync.dma_start(out=w2_sb[:].bitcast(I32), in_=w2_words.rearrange("b p n -> p b n").bitcast(I32))
+        for q in range(QUADRANTS):
             nc.sync.dma_start(
                 out=w2_sc[32 * q : 32 * q + 4, :, :].bitcast(I32),
-                in_=w2_scales[:, 4 * q : 4 * q + 4, :].rearrange("a r n -> r a n").bitcast(I32),
+                in_=w2_scales[:, 4 * q : 4 * q + 4, :].rearrange("b r n -> r b n").bitcast(I32),
             )
-        cast_w1(vcopy, 0, last, 0)
-        cast_w1(scopy, 0, last, 1)
-        quantize_w1(0, last, 0, 1)
-        project(0, 0, last)
-        quantize_w1(0, last, 1, 2)
-        project(0, 1, last)
-        empty_h(0, 0, (scopy, vcopy))
-        quantize_w1(0, last, 2, 4)
-        project(0, 2, last)
-        project(0, 3, last)
 
+        round_w1(vcopy, 0, LAST, 0)
+        round_w1(scopy, 0, LAST, 1)
+        quantize_w1(0, LAST, 0, 1)
+        project(0, 0, LAST)
+        quantize_w1(0, LAST, 1, 2)
+        project(0, 1, LAST)
+        empty_h(0, 0, (scopy, vcopy))
+        quantize_w1(0, LAST, 2, 4)
+        project(0, 2, LAST)
+        project(0, 3, LAST)
+
+        def prepare_second_half(copy, a, pair):
+            round_w1(copy, 1, a, pair)
+            quantize_w1(1, a, 2 * pair, 2 * pair + 2)
+
+        def tile_ready(b, t):
+            empty_h(b, t, (scopy, scopy))
+            receivers(b, t)
+
+        def first_half_edges(t):
+            sigmoid(0, t)
+            senders(0, t, 0, E)
+
+        receivers(0, 0)
         for t in range(1, PACK):
-            empty_h(0, t, (scopy, scopy))
-            receiver(0, t - 1)
-        receiver(0, PACK - 1)
-        for pair in range(2):
-            for a in range(PASSES1):
-                cast_w1(scopy, 1, a, pair)
-                quantize_w1(1, a, 2 * pair, 2 * pair + 2)
-            for t in range(2 * pair, 2 * pair + 2):
-                for a in range(PASSES1):
-                    project(1, t, a)
-                empty_h(1, t, (scopy, scopy if t == 0 else scopy))
+            tile_ready(0, t)
+        first_half_edges(0)
+        prepare_second_half(scopy, LAST, 0)
+        first_half_edges(1)
+        prepare_second_half(scopy, LAST, 1)
+        first_half_edges(2)
+        first_half_edges(3)
         for t in range(PACK):
-            sender(0, t, 0, E)
+            for a in range(PASSES):
+                project(1, t, a)
+
+        scale_first_half(0)
+        scale_first_half(1)
         for t in range(PACK):
-            receiver(1, t)
-        for part in range(3):
-            finish_v(0, 0, part * P, P)
-        quantize_z(0, 0, 0, 2 * P)
-        finish_s(0, 0, 3 * P, P)
-        parts = E // P
-        for part in range(parts):
+            tile_ready(1, t)
+        sigmoid(1, 0)
+        sigmoid(1, 1)
+        scale_first_half(2)
+        scale_first_half(3)
+        sigmoid(1, 2)
+        sigmoid(1, 3)
+
+        def second_half_senders(part):
             for t in range(PACK):
-                sender(1, t, part * P, P)
-            if part == 1:
-                quantize_z(0, 0, 2 * P, 2 * P)
-            (finish_s, finish_s, finish_v, finish_v)[part](1, part * P, 0, P)
-            quantize_z(1, part * P, 0, P)
-            if part == parts - 1:
-                last_messages(part * P)
-            else:
-                messages(part * P, 2 * (part % 2))
+                senders(1, t, part * PART, PART)
+
+        def first_half_z(part):
+            j0 = part * PART
+            scopy(*weave_views(0, j0, scaled[:, :, j0 : j0 + PART]))
+            quantize_z(0, j0)
+
+        def leave(part):
+            quantize_z(1, part * PART)
+            messages(part * PART, GROUPS * (part % 2))
+
+        second_half_senders(0)
+        second_half_senders(1)
+        finish_on_vector(0)
+        first_half_z(0)
+        finish_on_scalar(PART)
+        for part in range(1, E // PART):
+            first_half_z(part)
+        leave(0)
+        second_half_senders(2)
+        leave(1)
+        finish_on_vector(2 * PART)
+        leave(2)
+        second_half_senders(3)
+        finish_on_vector(3 * PART)
+        quantize_z(1, 3 * PART)
+        last_messages(3 * PART)

@@ -27,6 +27,7 @@ PASSES = K // K_PASS
 LAST = PASSES - 1
 HALVES = H // K_PASS
 PART = 128
+PIECE = PART // 2
 GROUP = 3
 GROUPS = N // P // GROUP
 RUN = 4
@@ -159,7 +160,11 @@ def tile_list_gated_edge_messages_kernel(
         def woven_tag(b, j0):
             return f"woven{b}_{j0}"
 
-        held_behind = {(1, 2 * PART): woven_tag(0, 0), (1, 3 * PART): woven_tag(0, 2 * PART)}
+        held_behind = {
+            (1, 2 * PART): woven_tag(0, 0),
+            (1, 3 * PART): woven_tag(0, 2 * PART),
+            (1, 3 * PART + PIECE): woven_tag(1, 2 * PART),
+        }
 
         def senders(b, t, j0, n):
             if (b, j0) not in gated:
@@ -175,7 +180,7 @@ def tile_list_gated_edge_messages_kernel(
         scaled = keep.tile([P, PACK, E], BF16, name="scaled", align_bytes=64)
 
         def weave_views(b, j0, tiles):
-            woven[b, j0] = keep.tile([P, PART * PACK], BF16, name=woven_tag(b, j0), align_bytes=64)
+            woven[b, j0] = keep.tile([P, tiles.shape[2] * PACK], BF16, name=woven_tag(b, j0), align_bytes=64)
             return (
                 woven[b, j0][:].rearrange("p (c i t) -> p c t i", i=RUN, t=PACK),
                 tiles.rearrange("p t (c i) -> p c t i", i=RUN),
@@ -183,7 +188,7 @@ def tile_list_gated_edge_messages_kernel(
 
         def finish_on_vector(j0):
             dst, src = weave_views(1, j0, gated[1, j0][:])
-            factor = gain_sb[:, 1, :].unsqueeze(1).unsqueeze(3).to_broadcast([P, PART // RUN, PACK, RUN])
+            factor = gain_sb[:, 1, :].unsqueeze(1).unsqueeze(3).to_broadcast(list(src.shape))
             nc.vector.tensor_tensor(dst, src, factor, MULT)
 
         def finish_on_scalar(j0):
@@ -195,10 +200,14 @@ def tile_list_gated_edge_messages_kernel(
         def scale_first_half(t):
             nc.scalar.activation(scaled[:, t, :], gated[0, 0][:, t, :], COPY, scale=gain_sb[:, 0, t : t + 1])
 
-        def quantize_z(b, j0):
-            z_codes[b, j0] = keep.tile([P, PART], U32, name=f"z_codes{b}_{j0}", align_bytes=64)
-            z_sc[b, j0] = keep.tile([P, PART], U8, name=f"z_sc{b}_{j0}", align_bytes=64)
-            nc.vector.quantize_mx(out=z_codes[b, j0][:].bitcast(FP8X4), scales=z_sc[b, j0][:], in_=woven[b, j0][:])
+        def quantize_z(b, j0, first=0, n=PART):
+            if first == 0:
+                z_codes[b, j0] = keep.tile([P, PART], U32, name=f"z_codes{b}_{j0}", align_bytes=64)
+                z_sc[b, j0] = keep.tile([P, PART], U8, name=f"z_sc{b}_{j0}", align_bytes=64)
+            cols = slice(first, first + n)
+            nc.vector.quantize_mx(
+                out=z_codes[b, j0][:, cols].bitcast(FP8X4), scales=z_sc[b, j0][:, cols], in_=woven[b, j0 + first][:]
+            )
 
         def message_pass(acc, nt, j0, b):
             nc.tensor.matmul_mx(
@@ -323,14 +332,20 @@ def tile_list_gated_edge_messages_kernel(
         finish_on_vector(0)
         first_half_z(0)
         finish_on_scalar(PART)
-        for part in range(1, E // PART):
-            first_half_z(part)
+        first_half_z(1)
+        first_half_z(2)
         leave(0)
+        first_half_z(3)
         second_half_senders(2)
         leave(1)
         finish_on_vector(2 * PART)
         leave(2)
-        second_half_senders(3)
-        finish_on_vector(3 * PART)
-        quantize_z(1, 3 * PART)
-        last_messages(3 * PART)
+
+        j0 = 3 * PART
+        for first in (0, PIECE):
+            for t in range(PACK):
+                senders(1, t, j0 + first, PIECE)
+        for first in (0, PIECE):
+            finish_on_vector(j0 + first)
+            quantize_z(1, j0, first, PIECE)
+        last_messages(j0)

@@ -27,10 +27,12 @@ PASSES = K // K_PASS
 LAST = PASSES - 1
 HALVES = H // K_PASS
 PART = 128
+PARTS = E // PART
 PIECE = PART // 2
 GROUP = 3
 GROUPS = N // P // GROUP
 RUN = 4
+FINISH_RUN = 2
 
 
 def tile_list_gated_edge_messages_kernel(
@@ -42,7 +44,6 @@ def tile_list_gated_edge_messages_kernel(
         keep = ctx.enter_context(tc.tile_pool(name="keep", bufs=1))
         raw_pool = ctx.enter_context(tc.tile_pool(name="raw", bufs=LAST))
         cast_pool = ctx.enter_context(tc.tile_pool(name="cast", bufs=3))
-        gate_pool = ctx.enter_context(tc.tile_pool(name="gate", bufs=6))
         psum = ctx.enter_context(tc.psum_pool(name="psum", bufs=1))
 
         offs_sb = keep.tile([P, S // LIST_COLUMN], U16, name="offs_sb")
@@ -148,104 +149,108 @@ def tile_list_gated_edge_messages_kernel(
             for side in range(2):
                 copies[side](h_sb[b][t][:, side * BANK : (side + 1) * BANK], h_ps[b, t, side][:])
 
-        gate, gated, woven, z_codes, z_sc = {}, {}, {}, {}, {}
+        gates, gated, scaled, z_codes, z_sc, acc = {}, {}, {}, {}, {}, {}
 
         def receivers(b, t):
-            gate[b, t] = gate_pool.tile([P, E], F32, name="gate")
-            nc.vector.tensor_copy(gate[b, t][:], h_sb[b][t][:].indirect(pos1_sb[:]))
+            nc.vector.tensor_copy(gates[b][:, t, :], h_sb[b][t][:].indirect(pos1_sb[:]))
+
+        def tile_ready(b, t):
+            empty_h(b, t, (scopy, scopy))
+            receivers(b, t)
 
         def sigmoid(b, t):
-            nc.scalar.activation(gate[b, t][:], gate[b, t][:], SIGMOID, bias=bg_sb[:, b, t : t + 1])
+            nc.scalar.activation(gates[b][:, t, :], gates[b][:, t, :], SIGMOID, bias=bg_sb[:, b, t : t + 1])
 
-        def woven_tag(b, j0):
-            return f"woven{b}_{j0}"
-
-        held_behind = {
-            (1, 2 * PART): woven_tag(0, 0),
-            (1, 3 * PART): woven_tag(0, 2 * PART),
-            (1, 3 * PART + PIECE): woven_tag(1, 2 * PART),
-        }
-
-        def senders(b, t, j0, n):
-            if (b, j0) not in gated:
-                tag = held_behind.get((b, j0), f"gated{b}_{j0}")
-                gated[b, j0] = keep.tile([P, PACK, n], F32, name=tag, align_bytes=64)
+        def senders(b, t, j0, dst):
+            n = dst.shape[1]
             nc.vector.tensor_tensor(
-                gated[b, j0][:, t, :],
+                dst,
                 h_sb[b][t][:].indirect(pos2_sb[:, j0 // LIST_COLUMN : (j0 + n) // LIST_COLUMN]),
-                gate[b, t][:, j0 : j0 + n],
+                gates[b][:, t, j0 : j0 + n],
                 MULT,
             )
 
-        scaled = keep.tile([P, PACK, E], BF16, name="scaled", align_bytes=64)
+        def aligned(shape, dtype, tag):
+            return keep.tile(shape, dtype, name=tag, align_bytes=64)
 
-        def weave_views(b, j0, tiles):
-            woven[b, j0] = keep.tile([P, tiles.shape[2] * PACK], BF16, name=woven_tag(b, j0), align_bytes=64)
+        def weave_views(dst, tiles, run):
             return (
-                woven[b, j0][:].rearrange("p (c i t) -> p c t i", i=RUN, t=PACK),
-                tiles.rearrange("p t (c i) -> p c t i", i=RUN),
+                dst.rearrange("p (c i t) -> p c t i", i=run, t=PACK),
+                tiles.rearrange("p t (c i) -> p c t i", i=run),
             )
 
-        def finish_on_vector(j0):
-            dst, src = weave_views(1, j0, gated[1, j0][:])
+        def finish_on_vector(dst, tiles):
+            dst, src = weave_views(dst, tiles, FINISH_RUN)
             factor = gain_sb[:, 1, :].unsqueeze(1).unsqueeze(3).to_broadcast(list(src.shape))
             nc.vector.tensor_tensor(dst, src, factor, MULT)
 
-        def finish_on_scalar(j0):
-            tiles = keep.tile([P, PACK, PART], BF16, name=f"scaled{j0}", align_bytes=64)
-            for t in range(PACK):
-                nc.scalar.activation(tiles[:, t, :], gated[1, j0][:, t, :], COPY, scale=gain_sb[:, 1, t : t + 1])
-            scopy(*weave_views(1, j0, tiles[:]))
+        def scale(b, t, src):
+            nc.scalar.activation(scaled[b][:, t, :], src[:, t, :], COPY, scale=gain_sb[:, b, t : t + 1])
 
-        def scale_first_half(t):
-            nc.scalar.activation(scaled[:, t, :], gated[0, 0][:, t, :], COPY, scale=gain_sb[:, 0, t : t + 1])
+        def weave(dst, tiles):
+            scopy(*weave_views(dst, tiles, RUN))
 
-        def quantize_z(b, j0, first=0, n=PART):
-            if first == 0:
-                z_codes[b, j0] = keep.tile([P, PART], U32, name=f"z_codes{b}_{j0}", align_bytes=64)
-                z_sc[b, j0] = keep.tile([P, PART], U8, name=f"z_sc{b}_{j0}", align_bytes=64)
-            cols = slice(first, first + n)
-            nc.vector.quantize_mx(
-                out=z_codes[b, j0][:, cols].bitcast(FP8X4), scales=z_sc[b, j0][:, cols], in_=woven[b, j0 + first][:]
-            )
+        def z_tiles(part, halves):
+            tag = f"{part}_{halves[0]}"
+            codes = aligned([P, len(halves) * PART], U32, f"z_codes{tag}")
+            plane = aligned([P, len(halves) * PART], U8, f"z_sc{tag}")
+            for i, b in enumerate(halves):
+                z_codes[b, part] = codes[:, i * PART : (i + 1) * PART]
+                z_sc[b, part] = plane[:, i * PART : (i + 1) * PART]
+            return codes[:], plane[:]
 
-        def message_pass(acc, nt, j0, b):
+        def quantize_z(codes, plane, woven):
+            nc.vector.quantize_mx(out=codes.bitcast(FP8X4), scales=plane, in_=woven)
+
+        def message_pass(nt, part, b, start, stop):
             nc.tensor.matmul_mx(
-                out=acc,
+                out=acc[part, nt],
                 lhsT=w2_sb[:, b, 2 * P * nt : 2 * P * (nt + 1)].bitcast(FP4X4),
                 lhsT_scale=w2_sc[:, b, P * nt : P * (nt + 1)],
-                rhs=z_codes[b, j0][:].bitcast(FP8X4),
-                rhs_scale=z_sc[b, j0][:],
-                start=(b == 0),
-                stop=(b == HALVES - 1),
+                rhs=z_codes[b, part].bitcast(FP8X4),
+                rhs_scale=z_sc[b, part],
+                start=start,
+                stop=stop,
             )
 
-        def store(res, nt, j0):
-            rows = out[nt * P : (nt + res.shape[1]) * P, j0 : j0 + PART]
+        banks = {}
+
+        def group_passes(part, g, b):
+            if b == 0:
+                banks[part, g] = psum.tile([P, GROUP, PART], F32, name=f"bank{GROUPS * (part % 2) + g}")
+            for u in range(GROUP):
+                acc[part, GROUP * g + u] = banks[part, g][:, u, :]
+                message_pass(GROUP * g + u, part, b, b == 0 and u == 0, b == HALVES - 1 and u == GROUP - 1)
+
+        def store(res, nt, part):
+            rows = out[nt * P : (nt + res.shape[1]) * P, part * PART : (part + 1) * PART]
             nc.sync.dma_start(out=rows.rearrange("(u p) j -> p u j", p=P), in_=res[:])
 
-        def messages(j0, first_bank):
+        def leave(part):
             for g in range(GROUPS):
-                acc = psum.tile([P, GROUP, PART], F32, name=f"bank{first_bank + g}")
-                for u in range(GROUP):
-                    for b in range(HALVES):
-                        message_pass(acc[:, u, :], GROUP * g + u, j0, b)
-                res = keep.tile([P, GROUP, PART], F32, name=f"res{j0}_{g}")
-                scopy(res[:], acc[:])
-                store(res, GROUP * g, j0)
+                res = keep.tile([P, GROUP, PART], F32, name=f"res{part}_{g}")
+                scopy(res[:], banks[part, g][:])
+                store(res, GROUP * g, part)
 
-        def last_messages(j0):
-            acc = [psum.tile([P, PART], F32, name=f"bank{GROUPS + nt}") for nt in range(N // P)]
-            res = [keep.tile([P, 1, PART], F32, name=f"res{j0}_{nt}") for nt in range(N // P)]
+        def messages(part):
+            for g in range(GROUPS):
+                for b in range(HALVES):
+                    group_passes(part, g, b)
+            leave(part)
+
+        def last_messages(part):
+            res = [keep.tile([P, 1, PART], F32, name=f"res{part}_{nt}") for nt in range(N // P)]
+            for nt in range(N // P):
+                acc[part, nt] = psum.tile([P, PART], F32, name=f"bank{GROUPS + nt}")[:]
             for b in range(HALVES):
                 for u in range(GROUP):
                     for g in range(GROUPS):
-                        message_pass(acc[GROUP * g + u][:], GROUP * g + u, j0, b)
+                        message_pass(GROUP * g + u, part, b, b == 0, b == HALVES - 1)
             for u in range(GROUP):
-                scopy(res[u][:, 0, :], acc[u][:])
-                vcopy(res[GROUP + u][:, 0, :], acc[GROUP + u][:])
-                store(res[u], u, j0)
-                store(res[GROUP + u], GROUP + u, j0)
+                scopy(res[u][:, 0, :], acc[part, u])
+                vcopy(res[GROUP + u][:, 0, :], acc[part, GROUP + u])
+                store(res[u], u, part)
+                store(res[GROUP + u], GROUP + u, part)
 
         gather_words(0)
         nc.vector.tensor_copy(v_sc[:], tab_sc[:].indirect(offs_sb[:]))
@@ -278,74 +283,82 @@ def tile_list_gated_edge_messages_kernel(
         project(0, 2, LAST)
         project(0, 3, LAST)
 
-        def prepare_second_half(copy, a, pair):
-            round_w1(copy, 1, a, pair)
-            quantize_w1(1, a, 2 * pair, 2 * pair + 2)
-
-        def tile_ready(b, t):
-            empty_h(b, t, (scopy, scopy))
-            receivers(b, t)
-
-        def first_half_edges(t):
-            sigmoid(0, t)
-            senders(0, t, 0, E)
-
+        gates[0] = keep.tile([P, PACK, E], F32, name="gates0")
+        gated[0] = aligned([P, PACK, E], F32, "gated0")
         receivers(0, 0)
         for t in range(1, PACK):
             tile_ready(0, t)
-        first_half_edges(0)
-        prepare_second_half(scopy, LAST, 0)
-        first_half_edges(1)
-        prepare_second_half(scopy, LAST, 1)
-        first_half_edges(2)
-        first_half_edges(3)
+        for t in range(PACK):
+            sigmoid(0, t)
+            senders(0, t, 0, gated[0][:, t, :])
+            if t < 2:
+                round_w1(scopy, 1, LAST, t)
+                quantize_w1(1, LAST, 2 * t, 2 * t + 2)
         for t in range(PACK):
             for a in range(PASSES):
                 project(1, t, a)
 
-        scale_first_half(0)
-        scale_first_half(1)
+        scaled[0] = aligned([P, PACK, E], BF16, "scaled0")
+        gates[1] = keep.tile([P, PACK, E], F32, name="raw0")
+        scale(0, 0, gated[0])
+        scale(0, 1, gated[0])
         for t in range(PACK):
             tile_ready(1, t)
         sigmoid(1, 0)
         sigmoid(1, 1)
-        scale_first_half(2)
-        scale_first_half(3)
+        scale(0, 2, gated[0])
         sigmoid(1, 2)
+        scale(0, 3, gated[0])
         sigmoid(1, 3)
 
-        def second_half_senders(part):
-            for t in range(PACK):
-                senders(1, t, part * PART, PART)
+        def edges(tiles, part):
+            return tiles[:, :, part * PART : (part + 1) * PART]
 
-        def first_half_z(part):
-            j0 = part * PART
-            scopy(*weave_views(0, j0, scaled[:, :, j0 : j0 + PART]))
-            quantize_z(0, j0)
-
-        def leave(part):
-            quantize_z(1, part * PART)
-            messages(part * PART, GROUPS * (part % 2))
-
-        second_half_senders(0)
-        second_half_senders(1)
-        finish_on_vector(0)
-        first_half_z(0)
-        finish_on_scalar(PART)
-        first_half_z(1)
-        first_half_z(2)
+        width = PART * PACK
+        early = aligned([P, PACK, 2 * PART], F32, "early")
+        for t in range(PACK):
+            senders(1, t, 0, early[:, t, :])
+        woven_10 = aligned([P, width], BF16, "woven_10")
+        finish_on_vector(woven_10[:], edges(early, 0))
+        woven_00 = aligned([P, width], BF16, "slot_a")
+        weave(woven_00[:], edges(scaled[0], 0))
+        quantize_z(*z_tiles(0, [0]), woven_00[:])
+        for g in range(GROUPS):
+            group_passes(0, g, 0)
+        woven_1 = aligned([P, HALVES * width], BF16, "slot_b")
+        woven_2 = aligned([P, HALVES * width], BF16, "woven_2")
+        scaled[1] = aligned([P, PACK, PART], BF16, "scaled1")
+        for t in range(PACK):
+            scale(1, t, edges(early, 1))
+        weave(woven_1[:, width:], scaled[1][:])
+        weave(woven_1[:, :width], edges(scaled[0], 1))
+        weave(woven_2[:, :width], edges(scaled[0], 2))
+        quantize_z(*z_tiles(0, [1]), woven_10[:])
+        for g in range(GROUPS):
+            group_passes(0, g, 1)
         leave(0)
-        first_half_z(3)
-        second_half_senders(2)
-        leave(1)
-        finish_on_vector(2 * PART)
-        leave(2)
+        woven_03 = aligned([P, width], BF16, "z_codes0_1")
+        weave(woven_03[:], edges(scaled[0], 3))
+        quantize_z(*z_tiles(3, [0]), woven_03[:])
 
-        j0 = 3 * PART
+        third = aligned([P, PACK, PART], F32, "slot_a")
+        for t in range(PACK):
+            senders(1, t, 2 * PART, third[:, t, :])
+        quantize_z(*z_tiles(1, [0, 1]), woven_1[:])
+        messages(1)
+        finish_on_vector(woven_2[:, width:], third[:])
+        quantize_z(*z_tiles(2, [0, 1]), woven_2[:])
+        messages(2)
+
+        fourth = aligned([P, PACK, PART], F32, "slot_b")
+        for t in range(PACK - 1):
+            senders(1, t, 3 * PART, fourth[:, t, :])
         for first in (0, PIECE):
-            for t in range(PACK):
-                senders(1, t, j0 + first, PIECE)
+            senders(1, PACK - 1, 3 * PART + first, fourth[:, PACK - 1, first : first + PIECE])
+        codes, plane = z_tiles(3, [1])
         for first in (0, PIECE):
-            finish_on_vector(j0 + first)
-            quantize_z(1, j0, first, PIECE)
-        last_messages(j0)
+            cols = slice(first, first + PIECE)
+            woven = aligned([P, PIECE * PACK], BF16, f"woven_13_{first}")
+            finish_on_vector(woven[:], fourth[:, :, cols])
+            quantize_z(codes[:, cols], plane[:, cols], woven[:])
+        last_messages(PARTS - 1)

@@ -28,6 +28,8 @@ LAST = PASSES - 1
 HALVES = H // K_PASS
 PART = 128
 PARTS = E // PART
+QUARTER = S // 4
+SHARE = 80
 PIECE = PART // 2
 GROUP = 3
 GROUPS = N // P // GROUP
@@ -42,8 +44,7 @@ def tile_list_gated_edge_messages_kernel(
     vcopy, scopy = nc.vector.tensor_copy, nc.scalar.copy
     with ExitStack() as ctx:
         keep = ctx.enter_context(tc.tile_pool(name="keep", bufs=1))
-        raw_pool = ctx.enter_context(tc.tile_pool(name="raw", bufs=LAST))
-        cast_pool = ctx.enter_context(tc.tile_pool(name="cast", bufs=3))
+        cast_pool = ctx.enter_context(tc.tile_pool(name="cast", bufs=2))
         psum = ctx.enter_context(tc.psum_pool(name="psum", bufs=1))
 
         offs_sb = keep.tile([P, S // LIST_COLUMN], U16, name="offs_sb")
@@ -58,7 +59,7 @@ def tile_list_gated_edge_messages_kernel(
         tab_sb = [keep.tile([P, T], I32, name=f"tab{a}", align_bytes=64) for a in range(PASSES)]
         v_codes = [keep.tile([P, S], U32, name=f"v_codes{a}", align_bytes=64) for a in range(PASSES)]
         v_sc = keep.tile([P, S], U8, name="v_sc", align_bytes=64)
-        h_sb = [[keep.tile([P, S], F32, name=f"h{b}_{t}") for t in range(PACK)] for b in range(HALVES)]
+        h_sb = [[keep.tile([P, S], F32, name=f"h0_{t}") for t in range(PACK)], []]
 
         nc.vector.memset(tab_sc[:].bitcast(I32), 0)
         nc.vector.memset(w2_sc[:].rearrange("p b n -> p (b n)").bitcast(I32), 0)
@@ -66,107 +67,138 @@ def tile_list_gated_edge_messages_kernel(
         nc.vector.memset(warm[:], 0.0)
         nc.scalar.activation(warm[:], warm[:], SIGMOID)
 
-        for q in range(QUADRANTS):
-            nc.gpsimd.dma_start(
-                out=tab_sc[32 * q : 32 * q + 4 * PASSES, :].bitcast(I32),
-                in_=tab_scales[:, 4 * q : 4 * q + 4, :].bitcast(I32),
-            )
+        def load_table_scales():
+            for q in range(QUADRANTS):
+                nc.gpsimd.dma_start(
+                    out=tab_sc[32 * q : 32 * q + 4 * PASSES, :].bitcast(I32),
+                    in_=tab_scales[:, 4 * q : 4 * q + 4, :].bitcast(I32),
+                )
 
         raw = {}
 
         def load_table(a):
             nc.sync.dma_start(out=tab_sb[a][:], in_=tab_words[a].rearrange("p t i -> p (t i)").bitcast(I32))
 
-        def load_w1_rows(a):
-            whole = raw_pool.tile([P, PACK, H], F32, name="raw")
-            rows = w1[a * K_PASS : (a + 1) * K_PASS, :]
-            nc.sync.dma_start(out=whole[:], in_=rows.rearrange("(p j) c -> p j c", j=PACK))
-            for b in range(HALVES):
-                raw[b, a] = whole[:, :, b * K_PASS : (b + 1) * K_PASS]
-
-        def load_w1_half(b, a):
-            piece = keep.tile([P, PACK, K_PASS], F32, name=f"raw{b}")
+        def load_w1(b, a):
+            piece = keep.tile([P, PACK, K_PASS], F32, name=f"raw{b}_{a}")
             rows = w1[a * K_PASS : (a + 1) * K_PASS, b * K_PASS : (b + 1) * K_PASS]
             nc.sync.dma_start(out=piece[:], in_=rows.rearrange("(p j) c -> p j c", j=PACK))
             raw[b, a] = piece[:]
 
         load_table(0)
+        load_table_scales()
         nc.sync.dma_start(offs_sb[:], offs)
-        load_w1_rows(0)
-        load_table(1)
-        load_w1_rows(1)
+        load_w1(0, 0)
         load_table(LAST)
-        load_w1_half(0, LAST)
+        load_w1(0, 1)
+        load_table(1)
+        load_w1(0, LAST)
         nc.sync.dma_start(pos1_sb[:], pos1)
-        nc.sync.dma_start(pos2_sb[:], pos2)
+        load_w1(1, 0)
         nc.sync.dma_start(out=bg_sb[:], in_=bg.rearrange("(b p t) -> p b t", p=P, t=PACK))
+        load_w1(1, 1)
+        nc.sync.dma_start(pos2_sb[:], pos2)
+        load_w1(1, LAST)
         nc.sync.dma_start(out=gain_sb[:], in_=gain.rearrange("(b p t) -> p b t", p=P, t=PACK))
+        nc.sync.dma_start(out=w2_sb[:].bitcast(I32), in_=w2_words.rearrange("b p n -> p b n").bitcast(I32))
+        for q in range(QUADRANTS):
+            nc.sync.dma_start(
+                out=w2_sc[32 * q : 32 * q + 4, :, :].bitcast(I32),
+                in_=w2_scales[:, 4 * q : 4 * q + 4, :].rearrange("b r n -> r b n").bitcast(I32),
+            )
 
-        grouped, w1_codes, w1_sc = {}, {}, {}
+        rounded, w1_codes, w1_sc = {}, {}, {}
 
-        def round_w1(copy, b, a, pair):
-            if (b, a) not in grouped:
-                pool, tag = (keep, "shared") if (b, a) == (1, LAST) else (cast_pool, "grouped")
-                grouped[b, a] = pool.tile([P, PACK, P, PACK], BF16, name=tag, align_bytes=64)
+        def round_w1(copy, b, a, pair, dst):
             ts = slice(2 * pair, 2 * pair + 2)
             src = raw[b, a].rearrange("p j (m t) -> p m j t", t=PACK)[:, :, :, ts]
-            dst = grouped[b, a][:].rearrange("p t m j -> p m j t")[:, :, :, ts]
-            copy(dst, src)
+            copy(dst.rearrange("p t m j -> p m j t"), src)
 
-        def quantize_w1(b, a, t0=0, t1=PACK):
+        def quantize_w1(b, a, t0, src):
             if (b, a) not in w1_codes:
-                tag = "shared" if (b, a) == (0, LAST) else f"w1_codes{b}_{a}"
-                w1_codes[b, a] = keep.tile([P, K_PASS], U32, name=tag, align_bytes=64)
+                w1_codes[b, a] = keep.tile([P, K_PASS], U32, name=f"w1_codes{b}_{a}", align_bytes=64)
                 w1_sc[b, a] = keep.tile([P, K_PASS], U8, name=f"w1_sc{b}_{a}", align_bytes=64)
-            cols = slice(t0 * P, t1 * P)
+            cols = slice(t0 * P, (t0 + src.shape[1]) * P)
             nc.vector.quantize_mx(
                 out=w1_codes[b, a][:, cols].bitcast(FP8X4),
                 scales=w1_sc[b, a][:, cols],
-                in_=grouped[b, a][:, t0:t1, :, :].rearrange("p t m j -> p (t m j)"),
+                in_=src.rearrange("p t m j -> p (t m j)"),
             )
 
-        def gather_words(a):
-            nc.vector.tensor_copy(v_codes[a][:], tab_sb[a][:].bitcast(U32).indirect(offs_sb[:]))
+        def first_half_piece(a):
+            piece = cast_pool.tile([P, PACK, P, PACK], BF16, name="grouped", align_bytes=64)
+            for pair in range(2):
+                round_w1(scopy, 0, a, pair, piece[:, 2 * pair : 2 * pair + 2, :, :])
+            quantize_w1(0, a, 0, piece[:])
+
+        def round_pair(copy, a, pair, tag=None):
+            rounded[a, pair] = keep.tile([P, 2, P, PACK], BF16, name=tag or f"pair{a}_{pair}", align_bytes=64)
+            round_w1(copy, 1, a, pair, rounded[a, pair][:])
+
+        def quantize_pair(a, pair):
+            quantize_w1(1, a, 2 * pair, rounded[a, pair][:])
+
+        def gather_words(a, first=0, n=S):
+            picks = offs_sb[:, first // LIST_COLUMN : (first + n) // LIST_COLUMN]
+            nc.vector.tensor_copy(v_codes[a][:, first : first + n], tab_sb[a][:].bitcast(U32).indirect(picks))
 
         h_ps = {}
 
-        def project(b, t, a):
-            for side in range(2):
-                if a == 0:
-                    h_ps[b, t, side] = psum.tile([P, BANK], F32, name=f"bank{2 * t + side}")
-                cols = slice(side * BANK, (side + 1) * BANK)
-                nc.tensor.matmul_mx(
-                    out=h_ps[b, t, side][:],
-                    lhsT=w1_codes[b, a][:, t * P : (t + 1) * P].bitcast(FP8X4),
-                    lhsT_scale=w1_sc[b, a][:, t * P : (t + 1) * P],
-                    rhs=v_codes[a][:, cols].bitcast(FP8X4),
-                    rhs_scale=v_sc[4 * a :, cols],
-                    start=(a == 0),
-                    stop=(a == LAST),
-                )
+        def h_banks(b, t):
+            if (b, t) == (0, 0):
+                return 0, QUARTER
+            return (2 * (t + 1)) % 8, BANK
 
-        def empty_h(b, t, copies):
-            for side in range(2):
-                copies[side](h_sb[b][t][:, side * BANK : (side + 1) * BANK], h_ps[b, t, side][:])
+        def project(b, t, a, side, closing=LAST):
+            first, width = h_banks(b, t)
+            opening = (b, t, side) not in h_ps
+            if opening:
+                h_ps[b, t, side] = psum.tile([P, width], F32, name=f"bank{first + side}")
+            cols = slice(side * width, (side + 1) * width)
+            nc.tensor.matmul_mx(
+                out=h_ps[b, t, side][:],
+                lhsT=w1_codes[b, a][:, t * P : (t + 1) * P].bitcast(FP8X4),
+                lhsT_scale=w1_sc[b, a][:, t * P : (t + 1) * P],
+                rhs=v_codes[a][:, cols].bitcast(FP8X4),
+                rhs_scale=v_sc[4 * a :, cols],
+                start=opening,
+                stop=(a == closing),
+            )
+
+        def project_tile(b, t, passes, closing=LAST):
+            for a in passes:
+                for side in range(S // h_banks(b, t)[1]):
+                    project(b, t, a, side, closing)
+
+        def empty_h(b, t, side, copy=scopy):
+            width = h_banks(b, t)[1]
+            copy(h_sb[b][t][:, side * width : (side + 1) * width], h_ps[b, t, side][:])
 
         gates, gated, scaled, z_codes, z_sc, acc = {}, {}, {}, {}, {}, {}
 
+        picked = {}
+
         def receivers(b, t):
-            nc.vector.tensor_copy(gates[b][:, t, :], h_sb[b][t][:].indirect(pos1_sb[:]))
+            if b == 0:
+                picked[b, t] = keep.tile([P, E], F32, name=f"picked{t}", align_bytes=64)[:]
+            else:
+                picked[b, t] = gates[b, t]
+            nc.vector.tensor_copy(picked[b, t], h_sb[b][t][:].indirect(pos1_sb[:]))
 
         def tile_ready(b, t):
-            empty_h(b, t, (scopy, scopy))
+            empty_h(b, t, 0)
+            empty_h(b, t, 1)
             receivers(b, t)
 
         def sigmoid(b, t):
-            nc.scalar.activation(gates[b][:, t, :], gates[b][:, t, :], SIGMOID, bias=bg_sb[:, b, t : t + 1])
+            nc.scalar.activation(gates[b, t], picked[b, t], SIGMOID, bias=bg_sb[:, b, t : t + 1])
 
         def senders(b, t, j0, dst):
             n = dst.shape[1]
             nc.vector.tensor_tensor(
                 dst,
                 h_sb[b][t][:].indirect(pos2_sb[:, j0 // LIST_COLUMN : (j0 + n) // LIST_COLUMN]),
-                gates[b][:, t, j0 : j0 + n],
+                gates[b, t][:, j0 : j0 + n],
                 MULT,
             )
 
@@ -185,7 +217,7 @@ def tile_list_gated_edge_messages_kernel(
             nc.vector.tensor_tensor(dst, src, factor, MULT)
 
         def scale(b, t, src):
-            nc.scalar.activation(scaled[b][:, t, :], src[:, t, :], COPY, scale=gain_sb[:, b, t : t + 1])
+            nc.scalar.activation(scaled[b][:, t, :], src, COPY, scale=gain_sb[:, b, t : t + 1])
 
         def weave(dst, tiles):
             scopy(*weave_views(dst, tiles, RUN))
@@ -217,7 +249,7 @@ def tile_list_gated_edge_messages_kernel(
 
         def group_passes(part, g, b):
             if b == 0:
-                banks[part, g] = psum.tile([P, GROUP, PART], F32, name=f"bank{GROUPS * (part % 2) + g}")
+                banks[part, g] = psum.tile([P, GROUP, PART], F32, name=f"bank{GROUPS * (part + 1) + g}")
             for u in range(GROUP):
                 acc[part, GROUP * g + u] = banks[part, g][:, u, :]
                 message_pass(GROUP * g + u, part, b, b == 0 and u == 0, b == HALVES - 1 and u == GROUP - 1)
@@ -241,7 +273,7 @@ def tile_list_gated_edge_messages_kernel(
         def last_messages(part):
             res = [keep.tile([P, 1, PART], F32, name=f"res{part}_{nt}") for nt in range(N // P)]
             for nt in range(N // P):
-                acc[part, nt] = psum.tile([P, PART], F32, name=f"bank{GROUPS + nt}")[:]
+                acc[part, nt] = psum.tile([P, PART], F32, name=f"bank{nt}")[:]
             for b in range(HALVES):
                 for u in range(GROUP):
                     for g in range(GROUPS):
@@ -254,61 +286,90 @@ def tile_list_gated_edge_messages_kernel(
 
         gather_words(0)
         nc.vector.tensor_copy(v_sc[:], tab_sc[:].indirect(offs_sb[:]))
-        for a in range(LAST):
-            round_w1(scopy, 0, a, 0)
-            round_w1(scopy, 0, a, 1)
-            quantize_w1(0, a)
-            for t in range(PACK):
-                project(0, t, a)
-            gather_words(a + 1)
-            round_w1(scopy, 1, a, 0)
-            round_w1(vcopy if a == LAST - 1 else scopy, 1, a, 1)
-            quantize_w1(1, a)
-        load_w1_half(1, LAST)
-        nc.sync.dma_start(out=w2_sb[:].bitcast(I32), in_=w2_words.rearrange("b p n -> p b n").bitcast(I32))
-        for q in range(QUADRANTS):
-            nc.sync.dma_start(
-                out=w2_sc[32 * q : 32 * q + 4, :, :].bitcast(I32),
-                in_=w2_scales[:, 4 * q : 4 * q + 4, :].rearrange("b r n -> r b n").bitcast(I32),
-            )
+        first_half_piece(0)
+        for t in range(PACK - 1):
+            project_tile(0, t, [0])
+        gather_words(LAST)
+        first_half_piece(1)
+        gather_words(1, 0, BANK)
+        for t, side in ((0, 0), (0, 1), (1, 0), (2, 0)):
+            project(0, t, 1, side)
+        gather_words(1, BANK, BANK)
+        project(0, 0, 1, 2)
+        project(0, 0, 1, 3)
 
-        round_w1(vcopy, 0, LAST, 0)
-        round_w1(scopy, 0, LAST, 1)
-        quantize_w1(0, LAST, 0, 1)
-        project(0, 0, LAST)
-        quantize_w1(0, LAST, 1, 2)
-        project(0, 1, LAST)
-        empty_h(0, 0, (scopy, vcopy))
-        quantize_w1(0, LAST, 2, 4)
-        project(0, 2, LAST)
-        project(0, 3, LAST)
+        last_pairs = [aligned([P, 2, P, PACK], BF16, f"last_pair{pair}") for pair in range(2)]
+        src = raw[0, LAST].rearrange("p j (m t) -> p m j t", t=PACK)[:, :, :, 0:2]
+        dst = last_pairs[0][:].rearrange("p t m j -> p m j t")
+        vcopy(dst[:, :SHARE], src[:, :SHARE])
+        scopy(dst[:, SHARE:], src[:, SHARE:])
+        quantize_w1(0, LAST, 0, last_pairs[0][:, 0:1])
+        project_tile(0, 0, [LAST])
+        round_w1(scopy, 0, LAST, 1, last_pairs[1][:])
+        quantize_w1(0, LAST, 1, last_pairs[0][:, 1:2])
+        project(0, 1, LAST, 0)
+        project(0, 1, LAST, 1, closing=1)
+        project(0, 1, 1, 1, closing=1)
+        for quarter, copy in enumerate((vcopy, scopy, vcopy, scopy)):
+            empty_h(0, 0, quarter, copy)
+        quantize_w1(0, LAST, 2, last_pairs[1][:])
+        project(0, 2, LAST, 0)
+        project(0, 2, LAST, 1, closing=1)
+        project(0, 2, 1, 1, closing=1)
+        project_tile(0, 3, range(PASSES))
 
-        gates[0] = keep.tile([P, PACK, E], F32, name="gates0")
-        gated[0] = aligned([P, PACK, E], F32, "gated0")
+        def gate_tiles(b, tiles, tag):
+            held = keep.tile([P, len(tiles), E], F32, name=tag)
+            for i, t in enumerate(tiles):
+                gates[b, t] = held[:, i, :]
+
+        gate_tiles(0, [0], "raw0_0")
+        gate_tiles(1, range(PACK), "raw0_1")
+
+        def first_senders(t, tag):
+            gated[t] = aligned([P, E], F32, tag)
+            senders(0, t, 0, gated[t][:])
+
         receivers(0, 0)
+        tile_ready(0, 1)
+        tile_ready(0, 2)
+        sigmoid(0, 0)
+        first_senders(0, "gated0")
+        round_pair(scopy, 0, 0, "w1_codes0_0")
+        quantize_pair(0, 0)
+        tile_ready(0, 3)
+        round_pair(scopy, 0, 1, "w1_codes0_1")
+        quantize_pair(0, 1)
+        round_pair(vcopy, 1, 0, "picked0")
+        round_pair(vcopy, 1, 1, f"w1_codes0_{LAST}")
+        quantize_pair(1, 0)
+        quantize_pair(1, 1)
+        for pair in range(2):
+            round_pair(scopy, LAST, pair)
+            quantize_pair(LAST, pair)
+        gate_tiles(0, [1, 2, 3], f"raw1_{LAST}")
         for t in range(1, PACK):
-            tile_ready(0, t)
-        for t in range(PACK):
             sigmoid(0, t)
-            senders(0, t, 0, gated[0][:, t, :])
-            if t < 2:
-                round_w1(scopy, 1, LAST, t)
-                quantize_w1(1, LAST, 2 * t, 2 * t + 2)
-        for t in range(PACK):
-            for a in range(PASSES):
-                project(1, t, a)
+            first_senders(t, f"gated{t}")
+        for tag in ("picked2", "picked1", "h1_2", "h1_3"):
+            h_sb[1].append(aligned([P, S], F32, tag))
+        project_tile(1, 0, range(PASSES))
+        project_tile(1, 1, [0, LAST, 1], closing=1)
+        project_tile(1, 2, [LAST, 0, 1], closing=1)
+        project_tile(1, 3, [LAST, 0, 1], closing=1)
 
-        scaled[0] = aligned([P, PACK, E], BF16, "scaled0")
-        gates[1] = keep.tile([P, PACK, E], F32, name="raw0")
-        scale(0, 0, gated[0])
-        scale(0, 1, gated[0])
-        for t in range(PACK):
-            tile_ready(1, t)
+        scaled[0] = aligned([P, PACK, E], BF16, f"pair{LAST}_1")
+        scale(0, 0, gated[0][:])
+        tile_ready(1, 0)
+        tile_ready(1, 1)
+        scale(0, 1, gated[1][:])
+        tile_ready(1, 2)
+        tile_ready(1, 3)
         sigmoid(1, 0)
         sigmoid(1, 1)
-        scale(0, 2, gated[0])
+        scale(0, 2, gated[2][:])
         sigmoid(1, 2)
-        scale(0, 3, gated[0])
+        scale(0, 3, gated[3][:])
         sigmoid(1, 3)
 
         def edges(tiles, part):
@@ -329,7 +390,7 @@ def tile_list_gated_edge_messages_kernel(
         woven_2 = aligned([P, HALVES * width], BF16, "woven_2")
         scaled[1] = aligned([P, PACK, PART], BF16, "scaled1")
         for t in range(PACK):
-            scale(1, t, edges(early, 1))
+            scale(1, t, edges(early, 1)[:, t, :])
         weave(woven_1[:, width:], scaled[1][:])
         weave(woven_1[:, :width], edges(scaled[0], 1))
         weave(woven_2[:, :width], edges(scaled[0], 2))

@@ -18,6 +18,7 @@ COPY = mybir.ActivationFunctionType.Copy
 SIGMOID = mybir.ActivationFunctionType.Sigmoid
 
 P = 128
+HALF_P = P // 2
 PACK = 4
 K_PASS = P * PACK
 BANK = 512
@@ -29,12 +30,14 @@ HALVES = H // K_PASS
 PART = 128
 PARTS = E // PART
 QUARTER = S // 4
-SHARE = 80
 PIECE = PART // 2
 GROUP = 3
 GROUPS = N // P // GROUP
 RUN = 4
 FINISH_RUN = 2
+W1_COLUMNS = ((0, 256), (256, 256), (512, 512))
+TILES = ((0, 0), (0, 1), (1, 0), (1, 1), (2, 0), (2, 1), (2, 2), (2, 3))
+LAID = {"raw1_1": 0, "gates0": 0, "gates1": 2048, "middle_low": 1024, "middle_high": 3072, "raw2_0": 5120, "h2": 5120, "h3": 9216, "raw2_2": 13312, "gates2": 13312, "gates3": 17408, "sent": 21504, "scaled": 24576, "res0": 22016, "woven_2": 25088, "rounded1_1": 29696, "rounded1_0": 30720, "rounded1_2": 31744, "picked0": 33792, "rounded2_0": 33792, "last_low": 33792, "last_high": 35840}
 
 
 def tile_list_gated_edge_messages_kernel(
@@ -44,22 +47,23 @@ def tile_list_gated_edge_messages_kernel(
     vcopy, scopy = nc.vector.tensor_copy, nc.scalar.copy
     with ExitStack() as ctx:
         keep = ctx.enter_context(tc.tile_pool(name="keep", bufs=1))
-        cast_pool = ctx.enter_context(tc.tile_pool(name="cast", bufs=2))
+        laid = ctx.enter_context(tc.tile_pool(name="laid", bufs=1))
         psum = ctx.enter_context(tc.psum_pool(name="psum", bufs=1))
+
+        def aligned(shape, dtype, tag):
+            if tag in LAID:
+                return laid.tile(shape, dtype, name=tag, align_bytes=64, offset=LAID[tag])
+            return keep.tile(shape, dtype, name=tag, align_bytes=64)
 
         offs_sb = keep.tile([P, S // LIST_COLUMN], U16, name="offs_sb")
         pos1_sb = keep.tile([P, E // LIST_COLUMN], U16, name="pos1_sb")
         pos2_sb = keep.tile([P, E // LIST_COLUMN], U16, name="pos2_sb")
-        tab_sc = keep.tile([P, T], U8, name="tab_sc", align_bytes=64)
-        w2_sc = keep.tile([P, HALVES, N], U8, name="w2_sc", align_bytes=64)
-        w2_sb = keep.tile([P, HALVES, 2 * N], U8, name="w2_sb", align_bytes=64)
-        bg_sb = keep.tile([P, HALVES, PACK], F32, name="bg_sb")
-        gain_sb = keep.tile([P, HALVES, PACK], F32, name="gain_sb")
-        warm = keep.tile([P, PACK], F32, name="warm")
-        tab_sb = [keep.tile([P, T], I32, name=f"tab{a}", align_bytes=64) for a in range(PASSES)]
-        v_codes = [keep.tile([P, S], U32, name=f"v_codes{a}", align_bytes=64) for a in range(PASSES)]
-        v_sc = keep.tile([P, S], U8, name="v_sc", align_bytes=64)
-        h_sb = [[keep.tile([P, S], F32, name=f"h0_{t}") for t in range(PACK)], []]
+        tab_sc = aligned([P, T], U8, "tab_sc")
+        w2_sc = aligned([P, HALVES, N], U8, "w2_sc")
+        w2_sb = aligned([P, HALVES, 2 * N], U8, "w2_sb")
+        warm = aligned([P, PACK], F32, "warm")
+        tab_sb = [aligned([P, T], I32, f"tab{a}") for a in range(PASSES)]
+        v_codes = [aligned([P, S], U32, f"v_codes{a}") for a in range(PASSES)]
 
         nc.vector.memset(tab_sc[:].bitcast(I32), 0)
         nc.vector.memset(w2_sc[:].rearrange("p b n -> p (b n)").bitcast(I32), 0)
@@ -76,29 +80,53 @@ def tile_list_gated_edge_messages_kernel(
 
         raw = {}
 
-        def load_table(a):
-            nc.sync.dma_start(out=tab_sb[a][:], in_=tab_words[a].rearrange("p t i -> p (t i)").bitcast(I32))
+        def load_table(a, pieces=1):
+            words = tab_words[a].rearrange("p t i -> p (t i)").bitcast(I32)
+            for first in range(0, T, T // pieces):
+                cols = slice(first, first + T // pieces)
+                nc.sync.dma_start(out=tab_sb[a][:, cols], in_=words[:, cols])
 
-        def load_w1(b, a):
-            piece = keep.tile([P, PACK, K_PASS], F32, name=f"raw{b}_{a}")
-            rows = w1[a * K_PASS : (a + 1) * K_PASS, b * K_PASS : (b + 1) * K_PASS]
+        def load_w1(g, a):
+            first, width = W1_COLUMNS[g]
+            piece = aligned([P, PACK, width], F32, f"raw{g}_{a}")
+            rows = w1[a * K_PASS : (a + 1) * K_PASS, first : first + width]
             nc.sync.dma_start(out=piece[:], in_=rows.rearrange("(p j) c -> p j c", j=PACK))
-            raw[b, a] = piece[:]
+            raw[g, a] = piece[:]
 
-        load_table(0)
+        def load_quarters(vec, tag):
+            held = aligned([P, 2, 8], F32, tag)
+            src = vec[0:K_PASS].rearrange("(q p t) -> p q t", p=HALF_P, t=PACK)
+            for side in range(2):
+                nc.sync.dma_start(
+                    out=held[side * HALF_P : (side + 1) * HALF_P, :, 0 : PACK - 1],
+                    in_=src[:, :, side : side + PACK - 1],
+                )
+            return [held[:, n // 2, 2 * (n % 2) : 2 * (n % 2) + 1] for n in range(PACK)]
+
+        def load_half(vec, tag):
+            held = aligned([P, PACK], F32, tag)
+            nc.sync.dma_start(out=held[:], in_=vec[K_PASS:].rearrange("(p t) -> p t", t=PACK))
+            return held
+
+        load_table(0, 4)
         load_table_scales()
         nc.sync.dma_start(offs_sb[:], offs)
+        load_table(1)
         load_w1(0, 0)
         load_table(LAST)
         load_w1(0, 1)
-        load_table(1)
         load_w1(0, LAST)
-        nc.sync.dma_start(pos1_sb[:], pos1)
         load_w1(1, 0)
-        nc.sync.dma_start(out=bg_sb[:], in_=bg.rearrange("(b p t) -> p b t", p=P, t=PACK))
+        nc.sync.dma_start(pos1_sb[:], pos1)
         load_w1(1, 1)
-        nc.sync.dma_start(pos2_sb[:], pos2)
         load_w1(1, LAST)
+        bias_first = load_quarters(bg, "bias_first")
+        nc.sync.dma_start(pos2_sb[:], pos2)
+        load_w1(2, 0)
+        load_w1(2, 1)
+        load_w1(2, LAST)
+        bias_second = load_half(bg, "bias_second")
+        gain_sb = aligned([P, HALVES, PACK], F32, "gain_sb")
         nc.sync.dma_start(out=gain_sb[:], in_=gain.rearrange("(b p t) -> p b t", p=P, t=PACK))
         nc.sync.dma_start(out=w2_sb[:].bitcast(I32), in_=w2_words.rearrange("b p n -> p b n").bitcast(I32))
         for q in range(QUADRANTS):
@@ -106,104 +134,97 @@ def tile_list_gated_edge_messages_kernel(
                 out=w2_sc[32 * q : 32 * q + 4, :, :].bitcast(I32),
                 in_=w2_scales[:, 4 * q : 4 * q + 4, :].rearrange("b r n -> r b n").bitcast(I32),
             )
+        bias = bias_first + [bias_second[:, t : t + 1] for t in range(PACK)]
+        factor = [gain_sb[:, n // PACK, n % PACK : n % PACK + 1] for n in range(2 * PACK)]
 
         rounded, w1_codes, w1_sc = {}, {}, {}
 
-        def round_w1(copy, b, a, pair, dst):
-            ts = slice(2 * pair, 2 * pair + 2)
-            src = raw[b, a].rearrange("p j (m t) -> p m j t", t=PACK)[:, :, :, ts]
-            copy(dst.rearrange("p t m j -> p m j t"), src)
+        def round_w1(copy, g, a, ts, tag):
+            width = W1_COLUMNS[g][1] // PACK
+            dst = aligned([P, len(ts), width, PACK], BF16, tag)
+            src = raw[g, a].rearrange("p j (m t) -> p m j t", t=PACK)
+            for i in range(0, len(ts), 2):
+                copy(dst[:, i : i + 2].rearrange("p t m j -> p m j t"), src[:, :, :, ts[i] : ts[i] + 2])
+            rounded[g, a, ts[0]] = dst[:].rearrange("p t m j -> p (t m j)")
 
-        def quantize_w1(b, a, t0, src):
-            if (b, a) not in w1_codes:
-                w1_codes[b, a] = keep.tile([P, K_PASS], U32, name=f"w1_codes{b}_{a}", align_bytes=64)
-                w1_sc[b, a] = keep.tile([P, K_PASS], U8, name=f"w1_sc{b}_{a}", align_bytes=64)
-            cols = slice(t0 * P, (t0 + src.shape[1]) * P)
+        def quantize_w1(g, a, t0):
+            width = W1_COLUMNS[g][1]
+            if (g, a) not in w1_codes:
+                w1_codes[g, a] = aligned([P, width], U32, f"w1_codes{g}_{a}")
+                w1_sc[g, a] = aligned([P, width], U8, f"w1_sc{g}_{a}")
+            src = rounded[g, a, t0]
+            first = t0 * width // PACK
+            cols = slice(first, first + src.shape[1] // PACK)
             nc.vector.quantize_mx(
-                out=w1_codes[b, a][:, cols].bitcast(FP8X4),
-                scales=w1_sc[b, a][:, cols],
-                in_=src.rearrange("p t m j -> p (t m j)"),
+                out=w1_codes[g, a][:, cols].bitcast(FP8X4), scales=w1_sc[g, a][:, cols], in_=src
             )
-
-        def first_half_piece(a):
-            piece = cast_pool.tile([P, PACK, P, PACK], BF16, name="grouped", align_bytes=64)
-            for pair in range(2):
-                round_w1(scopy, 0, a, pair, piece[:, 2 * pair : 2 * pair + 2, :, :])
-            quantize_w1(0, a, 0, piece[:])
-
-        def round_pair(copy, a, pair, tag=None):
-            rounded[a, pair] = keep.tile([P, 2, P, PACK], BF16, name=tag or f"pair{a}_{pair}", align_bytes=64)
-            round_w1(copy, 1, a, pair, rounded[a, pair][:])
-
-        def quantize_pair(a, pair):
-            quantize_w1(1, a, 2 * pair, rounded[a, pair][:])
 
         def gather_words(a, first=0, n=S):
             picks = offs_sb[:, first // LIST_COLUMN : (first + n) // LIST_COLUMN]
             nc.vector.tensor_copy(v_codes[a][:, first : first + n], tab_sb[a][:].bitcast(U32).indirect(picks))
 
-        h_ps = {}
+        h_ps, h_sb, planes = {}, {}, []
 
-        def h_banks(b, t):
-            if (b, t) == (0, 0):
+        def h_banks(n):
+            if n == 0:
                 return 0, QUARTER
-            return (2 * (t + 1)) % 8, BANK
+            return (2 * (n + 1)) % 8, BANK
 
-        def project(b, t, a, side, closing=LAST):
-            first, width = h_banks(b, t)
-            opening = (b, t, side) not in h_ps
+        def project(n, a, side, closing=LAST):
+            first, width = h_banks(n)
+            g, place = TILES[n]
+            opening = (n, side) not in h_ps
             if opening:
-                h_ps[b, t, side] = psum.tile([P, width], F32, name=f"bank{first + side}")
+                h_ps[n, side] = psum.tile([P, width], F32, name=f"bank{first + side}")
             cols = slice(side * width, (side + 1) * width)
             nc.tensor.matmul_mx(
-                out=h_ps[b, t, side][:],
-                lhsT=w1_codes[b, a][:, t * P : (t + 1) * P].bitcast(FP8X4),
-                lhsT_scale=w1_sc[b, a][:, t * P : (t + 1) * P],
+                out=h_ps[n, side][:],
+                lhsT=w1_codes[g, a][:, place * P : (place + 1) * P].bitcast(FP8X4),
+                lhsT_scale=w1_sc[g, a][:, place * P : (place + 1) * P],
                 rhs=v_codes[a][:, cols].bitcast(FP8X4),
-                rhs_scale=v_sc[4 * a :, cols],
+                rhs_scale=planes[0][4 * a :, cols],
                 start=opening,
                 stop=(a == closing),
             )
 
-        def project_tile(b, t, passes, closing=LAST):
+        def project_tile(n, passes, closing=LAST):
             for a in passes:
-                for side in range(S // h_banks(b, t)[1]):
-                    project(b, t, a, side, closing)
+                for side in range(S // h_banks(n)[1]):
+                    project(n, a, side, closing)
 
-        def empty_h(b, t, side, copy=scopy):
-            width = h_banks(b, t)[1]
-            copy(h_sb[b][t][:, side * width : (side + 1) * width], h_ps[b, t, side][:])
+        def empty_h(n, side, copy=scopy, tag=None):
+            if n not in h_sb:
+                h_sb[n] = aligned([P, S], F32, tag or f"h{n}")
+            width = h_banks(n)[1]
+            copy(h_sb[n][:, side * width : (side + 1) * width], h_ps[n, side][:])
 
-        gates, gated, scaled, z_codes, z_sc, acc = {}, {}, {}, {}, {}, {}
+        def empty_tile(n, tag=None):
+            empty_h(n, 0, tag=tag)
+            empty_h(n, 1)
 
-        picked = {}
+        gates, picked, gated, z_codes, z_sc, acc = {}, {}, {}, {}, {}, {}
 
-        def receivers(b, t):
-            if b == 0:
-                picked[b, t] = keep.tile([P, E], F32, name=f"picked{t}", align_bytes=64)[:]
-            else:
-                picked[b, t] = gates[b, t]
-            nc.vector.tensor_copy(picked[b, t], h_sb[b][t][:].indirect(pos1_sb[:]))
+        def receivers(n, tag=None):
+            if n not in picked:
+                picked[n] = aligned([P, E], F32, tag or f"picked{n}")[:]
+            nc.vector.tensor_copy(picked[n], h_sb[n][:].indirect(pos1_sb[:]))
 
-        def tile_ready(b, t):
-            empty_h(b, t, 0)
-            empty_h(b, t, 1)
-            receivers(b, t)
+        def sigmoid(n, tag=None):
+            gates[n] = aligned([P, E], F32, tag)[:] if tag else picked[n]
+            nc.scalar.activation(gates[n], picked[n], SIGMOID, bias=bias[n])
 
-        def sigmoid(b, t):
-            nc.scalar.activation(gates[b, t], picked[b, t], SIGMOID, bias=bg_sb[:, b, t : t + 1])
-
-        def senders(b, t, j0, dst):
-            n = dst.shape[1]
+        def senders(n, j0, dst):
+            width = dst.shape[1]
             nc.vector.tensor_tensor(
                 dst,
-                h_sb[b][t][:].indirect(pos2_sb[:, j0 // LIST_COLUMN : (j0 + n) // LIST_COLUMN]),
-                gates[b, t][:, j0 : j0 + n],
+                h_sb[n][:].indirect(pos2_sb[:, j0 // LIST_COLUMN : (j0 + width) // LIST_COLUMN]),
+                gates[n][:, j0 : j0 + width],
                 MULT,
             )
 
-        def aligned(shape, dtype, tag):
-            return keep.tile(shape, dtype, name=tag, align_bytes=64)
+        def first_senders(n, tag=None):
+            gated[n] = aligned([P, E], F32, tag or f"gated{n}")[:]
+            senders(n, 0, gated[n])
 
         def weave_views(dst, tiles, run):
             return (
@@ -213,11 +234,11 @@ def tile_list_gated_edge_messages_kernel(
 
         def finish_on_vector(dst, tiles):
             dst, src = weave_views(dst, tiles, FINISH_RUN)
-            factor = gain_sb[:, 1, :].unsqueeze(1).unsqueeze(3).to_broadcast(list(src.shape))
-            nc.vector.tensor_tensor(dst, src, factor, MULT)
+            factors = gain_sb[:, 1, :].unsqueeze(1).unsqueeze(3).to_broadcast(list(src.shape))
+            nc.vector.tensor_tensor(dst, src, factors, MULT)
 
-        def scale(b, t, src):
-            nc.scalar.activation(scaled[b][:, t, :], src, COPY, scale=gain_sb[:, b, t : t + 1])
+        def scale(n, dst, src):
+            nc.scalar.activation(dst, src, COPY, scale=factor[n])
 
         def weave(dst, tiles):
             scopy(*weave_views(dst, tiles, RUN))
@@ -256,13 +277,13 @@ def tile_list_gated_edge_messages_kernel(
 
         def store(res, nt, part):
             rows = out[nt * P : (nt + res.shape[1]) * P, part * PART : (part + 1) * PART]
-            nc.sync.dma_start(out=rows.rearrange("(u p) j -> p u j", p=P), in_=res[:])
+            nc.sync.dma_start(out=rows.rearrange("(u p) j -> p u j", p=P), in_=res)
 
-        def leave(part):
+        def leave(part, tag=None):
+            res = aligned([P, GROUPS, GROUP, PART], F32, tag or f"res{part}")
             for g in range(GROUPS):
-                res = keep.tile([P, GROUP, PART], F32, name=f"res{part}_{g}")
-                scopy(res[:], banks[part, g][:])
-                store(res, GROUP * g, part)
+                scopy(res[:, g], banks[part, g][:])
+                store(res[:, g], GROUP * g, part)
 
         def messages(part):
             for g in range(GROUPS):
@@ -271,7 +292,7 @@ def tile_list_gated_edge_messages_kernel(
             leave(part)
 
         def last_messages(part):
-            res = [keep.tile([P, 1, PART], F32, name=f"res{part}_{nt}") for nt in range(N // P)]
+            res = [aligned([P, 1, PART], F32, f"res{part}_{nt}") for nt in range(N // P)]
             for nt in range(N // P):
                 acc[part, nt] = psum.tile([P, PART], F32, name=f"bank{nt}")[:]
             for b in range(HALVES):
@@ -281,141 +302,140 @@ def tile_list_gated_edge_messages_kernel(
             for u in range(GROUP):
                 scopy(res[u][:, 0, :], acc[part, u])
                 vcopy(res[GROUP + u][:, 0, :], acc[part, GROUP + u])
-                store(res[u], u, part)
-                store(res[GROUP + u], GROUP + u, part)
+                store(res[u][:], u, part)
+                store(res[GROUP + u][:], GROUP + u, part)
 
-        gather_words(0)
-        nc.vector.tensor_copy(v_sc[:], tab_sc[:].indirect(offs_sb[:]))
-        first_half_piece(0)
-        for t in range(PACK - 1):
-            project_tile(0, t, [0])
-        gather_words(LAST)
-        first_half_piece(1)
-        gather_words(1, 0, BANK)
-        for t, side in ((0, 0), (0, 1), (1, 0), (2, 0)):
-            project(0, t, 1, side)
-        gather_words(1, BANK, BANK)
-        project(0, 0, 1, 2)
-        project(0, 0, 1, 3)
-
-        last_pairs = [aligned([P, 2, P, PACK], BF16, f"last_pair{pair}") for pair in range(2)]
-        src = raw[0, LAST].rearrange("p j (m t) -> p m j t", t=PACK)[:, :, :, 0:2]
-        dst = last_pairs[0][:].rearrange("p t m j -> p m j t")
-        vcopy(dst[:, :SHARE], src[:, :SHARE])
-        scopy(dst[:, SHARE:], src[:, SHARE:])
-        quantize_w1(0, LAST, 0, last_pairs[0][:, 0:1])
-        project_tile(0, 0, [LAST])
-        round_w1(scopy, 0, LAST, 1, last_pairs[1][:])
-        quantize_w1(0, LAST, 1, last_pairs[0][:, 1:2])
-        project(0, 1, LAST, 0)
-        project(0, 1, LAST, 1, closing=1)
-        project(0, 1, 1, 1, closing=1)
-        for quarter, copy in enumerate((vcopy, scopy, vcopy, scopy)):
-            empty_h(0, 0, quarter, copy)
-        quantize_w1(0, LAST, 2, last_pairs[1][:])
-        project(0, 2, LAST, 0)
-        project(0, 2, LAST, 1, closing=1)
-        project(0, 2, 1, 1, closing=1)
-        project_tile(0, 3, range(PASSES))
-
-        def gate_tiles(b, tiles, tag):
-            held = keep.tile([P, len(tiles), E], F32, name=tag)
-            for i, t in enumerate(tiles):
-                gates[b, t] = held[:, i, :]
-
-        gate_tiles(0, [0], "raw0_0")
-        gate_tiles(1, range(PACK), "raw0_1")
-
-        def first_senders(t, tag):
-            gated[t] = aligned([P, E], F32, tag)
-            senders(0, t, 0, gated[t][:])
-
-        receivers(0, 0)
-        tile_ready(0, 1)
-        tile_ready(0, 2)
-        sigmoid(0, 0)
-        first_senders(0, "gated0")
-        round_pair(scopy, 0, 0, "w1_codes0_0")
-        quantize_pair(0, 0)
-        tile_ready(0, 3)
-        round_pair(scopy, 0, 1, "w1_codes0_1")
-        quantize_pair(0, 1)
-        round_pair(vcopy, 1, 0, "picked0")
-        round_pair(vcopy, 1, 1, f"w1_codes0_{LAST}")
-        quantize_pair(1, 0)
-        quantize_pair(1, 1)
-        for pair in range(2):
-            round_pair(scopy, LAST, pair)
-            quantize_pair(LAST, pair)
-        gate_tiles(0, [1, 2, 3], f"raw1_{LAST}")
-        for t in range(1, PACK):
-            sigmoid(0, t)
-            first_senders(t, f"gated{t}")
-        for tag in ("picked2", "picked1", "h1_2", "h1_3"):
-            h_sb[1].append(aligned([P, S], F32, tag))
-        project_tile(1, 0, range(PASSES))
-        project_tile(1, 1, [0, LAST, 1], closing=1)
-        project_tile(1, 2, [LAST, 0, 1], closing=1)
-        project_tile(1, 3, [LAST, 0, 1], closing=1)
-
-        scaled[0] = aligned([P, PACK, E], BF16, f"pair{LAST}_1")
-        scale(0, 0, gated[0][:])
-        tile_ready(1, 0)
-        tile_ready(1, 1)
-        scale(0, 1, gated[1][:])
-        tile_ready(1, 2)
-        tile_ready(1, 3)
-        sigmoid(1, 0)
-        sigmoid(1, 1)
-        scale(0, 2, gated[2][:])
-        sigmoid(1, 2)
-        scale(0, 3, gated[3][:])
-        sigmoid(1, 3)
+        ALL, LOW, HIGH = (0, 1, 2, 3), (0, 1), (2, 3)
+        lo, hi = slice(0, HALF_P), slice(HALF_P, P)
 
         def edges(tiles, part):
             return tiles[:, :, part * PART : (part + 1) * PART]
 
+        gather_words(0)
+        gather_words(1)
+        round_w1(scopy, 0, 0, ALL, "rounded0_0")
+        quantize_w1(0, 0, 0)
+        planes.append(aligned([P, S], U8, "rounded0_0"))
+        nc.vector.tensor_copy(planes[0][:], tab_sc[:].indirect(offs_sb[:]))
+        project_tile(0, [0])
+        project_tile(1, [0])
+        gather_words(LAST)
+        round_w1(scopy, 0, 1, ALL, "rounded0_1")
+        quantize_w1(0, 1, 0)
+        project_tile(0, [1])
+        round_w1(scopy, 0, LAST, LOW, "rounded0_low")
+        round_w1(scopy, 0, LAST, HIGH, "rounded0_high")
+        quantize_w1(0, LAST, 0)
+        project_tile(0, [LAST])
+        quantize_w1(0, LAST, 2)
+        for side in range(2):
+            for a in (LAST, 1):
+                project(1, a, side, closing=1)
+        round_w1(scopy, 1, 0, ALL, "rounded1_0")
+        for quarter, copy in enumerate((vcopy, vcopy, vcopy, scopy)):
+            empty_h(0, quarter, copy)
+        receivers(0)
+        quantize_w1(1, 0, 0)
+        project_tile(2, [0])
+        empty_tile(1)
+        receivers(1)
+        project_tile(3, [0])
+        round_w1(scopy, 1, 1, ALL, "rounded1_1")
+        quantize_w1(1, 1, 0)
+        project_tile(2, [1])
+        project_tile(3, [1])
+        round_w1(vcopy, 1, LAST, ALL, "rounded1_2")
+        sent = aligned([P, PACK, E], F32, "sent")
+        parked = aligned([P, 2, E], F32, "parked")
+        sigmoid(0, "gates0")
+        senders(0, 0, sent[:, 0, :])
+        quantize_w1(1, LAST, 0)
+        project_tile(2, [LAST])
+        project_tile(3, [LAST])
+        sigmoid(1, "gates1")
+        senders(1, 0, sent[:, 2, :])
+        nc.sync.dma_start(out=sent[lo, 1::2, :], in_=sent[hi, 0::2, :])
+        round_w1(scopy, 2, 0, ALL, "rounded2_0")
+        quantize_w1(2, 0, 0)
+        round_w1(vcopy, 2, 1, LOW, "middle_low")
+        round_w1(vcopy, 2, 1, HIGH, "middle_high")
+        empty_tile(2)
+        receivers(2)
+        quantize_w1(2, 1, 0)
+        quantize_w1(2, 1, 2)
+        empty_tile(3)
+        receivers(3)
+        round_w1(scopy, 2, LAST, LOW, "last_low")
+        round_w1(scopy, 2, LAST, HIGH, "last_high")
+        quantize_w1(2, LAST, 0)
+        quantize_w1(2, LAST, 2)
+        for n in range(PACK, 2 * PACK):
+            project_tile(n, range(PASSES))
+        for n in (2, 3):
+            sigmoid(n, f"gates{n}")
+            senders(n, 0, parked[:, n - 2, :])
+            nc.sync.dma_start(out=sent[hi, 2 * n - 4, :], in_=parked[lo, n - 2, :])
+            nc.sync.dma_start(out=sent[hi, 2 * n - 3, :], in_=parked[hi, n - 2, :])
+        first_z = aligned([P, PACK, E], BF16, "first_z")
+        second = aligned([P, PACK, E], F32, "tab0")
+        for t, tag in enumerate(("picked2", "picked3", None, None)):
+            picked[PACK + t] = second[:, t, :]
+            empty_tile(PACK + t, tag)
+            receivers(PACK + t)
+            if t == 2:
+                scale(0, first_z[:, 0, :], sent[:, 0, :])
+        early = aligned([P, PACK, 2 * PART], F32, "tab2")
+
+        def gate_and_send(t):
+            sigmoid(PACK + t)
+            senders(PACK + t, 0, early[:, t, :])
+
+        gate_and_send(0)
+        gate_and_send(1)
+        scale(1, first_z[:, 1, :], sent[:, 1, :])
+        gate_and_send(2)
+        scale(2, first_z[:, 2, :], sent[:, 2, :])
+        gate_and_send(3)
+        scale(3, first_z[:, 3, :], sent[:, 3, :])
+
         width = PART * PACK
-        early = aligned([P, PACK, 2 * PART], F32, "early")
-        for t in range(PACK):
-            senders(1, t, 0, early[:, t, :])
         woven_10 = aligned([P, width], BF16, "woven_10")
         finish_on_vector(woven_10[:], edges(early, 0))
         woven_00 = aligned([P, width], BF16, "slot_a")
-        weave(woven_00[:], edges(scaled[0], 0))
+        weave(woven_00[:], edges(first_z, 0))
         quantize_z(*z_tiles(0, [0]), woven_00[:])
         for g in range(GROUPS):
             group_passes(0, g, 0)
         woven_1 = aligned([P, HALVES * width], BF16, "slot_b")
         woven_2 = aligned([P, HALVES * width], BF16, "woven_2")
-        scaled[1] = aligned([P, PACK, PART], BF16, "scaled1")
+        scaled = aligned([P, PACK, PART], BF16, "scaled")
         for t in range(PACK):
-            scale(1, t, edges(early, 1)[:, t, :])
-        weave(woven_1[:, width:], scaled[1][:])
-        weave(woven_1[:, :width], edges(scaled[0], 1))
-        weave(woven_2[:, :width], edges(scaled[0], 2))
+            scale(PACK + t, scaled[:, t, :], edges(early, 1)[:, t, :])
+        weave(woven_1[:, :width], edges(first_z, 1))
+        weave(woven_1[:, width:], scaled[:])
+        weave(woven_2[:, :width], edges(first_z, 2))
         quantize_z(*z_tiles(0, [1]), woven_10[:])
         for g in range(GROUPS):
             group_passes(0, g, 1)
         leave(0)
-        woven_03 = aligned([P, width], BF16, "z_codes0_1")
-        weave(woven_03[:], edges(scaled[0], 3))
-        quantize_z(*z_tiles(3, [0]), woven_03[:])
+        woven_03 = aligned([P, width], BF16, "woven_03")
+        weave(woven_03[:], edges(first_z, 3))
 
-        third = aligned([P, PACK, PART], F32, "slot_a")
+        third = aligned([P, PACK, PART], F32, "tab2")
         for t in range(PACK):
-            senders(1, t, 2 * PART, third[:, t, :])
+            senders(PACK + t, 2 * PART, third[:, t, :])
         quantize_z(*z_tiles(1, [0, 1]), woven_1[:])
         messages(1)
         finish_on_vector(woven_2[:, width:], third[:])
+        quantize_z(*z_tiles(3, [0]), woven_03[:])
         quantize_z(*z_tiles(2, [0, 1]), woven_2[:])
         messages(2)
 
         fourth = aligned([P, PACK, PART], F32, "slot_b")
         for t in range(PACK - 1):
-            senders(1, t, 3 * PART, fourth[:, t, :])
+            senders(PACK + t, 3 * PART, fourth[:, t, :])
         for first in (0, PIECE):
-            senders(1, PACK - 1, 3 * PART + first, fourth[:, PACK - 1, first : first + PIECE])
+            senders(2 * PACK - 1, 3 * PART + first, fourth[:, PACK - 1, first : first + PIECE])
         codes, plane = z_tiles(3, [1])
         for first in (0, PIECE):
             cols = slice(first, first + PIECE)

from contextlib import ExitStack

import concourse.mybir as mybir

K, T, S, E, H, N = 1536, 4096, 1024, 512, 1024, 768
FLOPS = 2 * K * H * S + 2 * H * N * E

F32 = mybir.dt.float32
BF16 = mybir.dt.bfloat16
I32 = mybir.dt.int32
U32 = mybir.dt.uint32
U16 = mybir.dt.uint16
U8 = mybir.dt.uint8
FP8X4 = mybir.dt.float8_e4m3fn_x4
FP4X4 = mybir.dt.float4_e2m1fn_x4
MULT = mybir.AluOpType.mult
COPY = mybir.ActivationFunctionType.Copy
SIGMOID = mybir.ActivationFunctionType.Sigmoid

P = 128
HALF_P = P // 2
PACK = 4
K_PASS = P * PACK
BANK = 512
QUADRANTS = 4
LIST_COLUMN = 16
PASSES = K // K_PASS
LAST = PASSES - 1
HALVES = H // K_PASS
PART = 128
PARTS = E // PART
QUARTER = S // 4
PIECE = PART // 2
GROUP = 3
GROUPS = N // P // GROUP
RUN = 4
FINISH_RUN = 2
W1_COLUMNS = ((0, 256), (256, 256), (512, 512))
TILES = ((0, 0), (0, 1), (1, 0), (1, 1), (2, 0), (2, 1), (2, 2), (2, 3))
LAID = {"raw1_1": 0, "gates0": 0, "gates1": 2048, "middle_low": 1024, "middle_high": 3072, "raw2_0": 5120, "h2": 5120, "h3": 9216, "raw2_2": 13312, "gates2": 13312, "gates3": 17408, "sent": 21504, "scaled": 24576, "res0": 22016, "woven_2": 25088, "rounded1_1": 29696, "rounded1_0": 30720, "rounded1_2": 31744, "picked0": 33792, "rounded2_0": 33792, "last_low": 33792, "last_high": 35840}


def tile_list_gated_edge_messages_kernel(
    tc, tab_words, tab_scales, offs, pos1, pos2, w1, bg, gain, w2_words, w2_scales, out
):
    nc = tc.nc
    vcopy, scopy = nc.vector.tensor_copy, nc.scalar.copy
    with ExitStack() as ctx:
        keep = ctx.enter_context(tc.tile_pool(name="keep", bufs=1))
        laid = ctx.enter_context(tc.tile_pool(name="laid", bufs=1))
        psum = ctx.enter_context(tc.psum_pool(name="psum", bufs=1))

        def aligned(shape, dtype, tag):
            if tag in LAID:
                return laid.tile(shape, dtype, name=tag, align_bytes=64, offset=LAID[tag])
            return keep.tile(shape, dtype, name=tag, align_bytes=64)

        offs_sb = keep.tile([P, S // LIST_COLUMN], U16, name="offs_sb")
        pos1_sb = keep.tile([P, E // LIST_COLUMN], U16, name="pos1_sb")
        pos2_sb = keep.tile([P, E // LIST_COLUMN], U16, name="pos2_sb")
        tab_sc = aligned([P, T], U8, "tab_sc")
        w2_sc = aligned([P, HALVES, N], U8, "w2_sc")
        w2_sb = aligned([P, HALVES, 2 * N], U8, "w2_sb")
        warm = aligned([P, PACK], F32, "warm")
        tab_sb = [aligned([P, T], I32, f"tab{a}") for a in range(PASSES)]
        v_codes = [aligned([P, S], U32, f"v_codes{a}") for a in range(PASSES)]

        nc.vector.memset(tab_sc[:].bitcast(I32), 0)
        nc.vector.memset(w2_sc[:].rearrange("p b n -> p (b n)").bitcast(I32), 0)

        nc.vector.memset(warm[:], 0.0)
        nc.scalar.activation(warm[:], warm[:], SIGMOID)

        def load_table_scales():
            for q in range(QUADRANTS):
                nc.gpsimd.dma_start(
                    out=tab_sc[32 * q : 32 * q + 4 * PASSES, :].bitcast(I32),
                    in_=tab_scales[:, 4 * q : 4 * q + 4, :].bitcast(I32),
                )

        raw = {}

        def load_table(a, pieces=1):
            words = tab_words[a].rearrange("p t i -> p (t i)").bitcast(I32)
            for first in range(0, T, T // pieces):
                cols = slice(first, first + T // pieces)
                nc.sync.dma_start(out=tab_sb[a][:, cols], in_=words[:, cols])

        def load_w1(g, a):
            first, width = W1_COLUMNS[g]
            piece = aligned([P, PACK, width], F32, f"raw{g}_{a}")
            rows = w1[a * K_PASS : (a + 1) * K_PASS, first : first + width]
            nc.sync.dma_start(out=piece[:], in_=rows.rearrange("(p j) c -> p j c", j=PACK))
            raw[g, a] = piece[:]

        def load_quarters(vec, tag):
            held = aligned([P, 2, 8], F32, tag)
            src = vec[0:K_PASS].rearrange("(q p t) -> p q t", p=HALF_P, t=PACK)
            for side in range(2):
                nc.sync.dma_start(
                    out=held[side * HALF_P : (side + 1) * HALF_P, :, 0 : PACK - 1],
                    in_=src[:, :, side : side + PACK - 1],
                )
            return [held[:, n // 2, 2 * (n % 2) : 2 * (n % 2) + 1] for n in range(PACK)]

        def load_half(vec, tag):
            held = aligned([P, PACK], F32, tag)
            nc.sync.dma_start(out=held[:], in_=vec[K_PASS:].rearrange("(p t) -> p t", t=PACK))
            return held

        load_table(0, 4)
        load_table_scales()
        nc.sync.dma_start(offs_sb[:], offs)
        load_table(1)
        load_w1(0, 0)
        load_table(LAST)
        load_w1(0, 1)
        load_w1(0, LAST)
        load_w1(1, 0)
        nc.sync.dma_start(pos1_sb[:], pos1)
        load_w1(1, 1)
        load_w1(1, LAST)
        bias_first = load_quarters(bg, "bias_first")
        nc.sync.dma_start(pos2_sb[:], pos2)
        load_w1(2, 0)
        load_w1(2, 1)
        load_w1(2, LAST)
        bias_second = load_half(bg, "bias_second")
        gain_sb = aligned([P, HALVES, PACK], F32, "gain_sb")
        nc.sync.dma_start(out=gain_sb[:], in_=gain.rearrange("(b p t) -> p b t", p=P, t=PACK))
        nc.sync.dma_start(out=w2_sb[:].bitcast(I32), in_=w2_words.rearrange("b p n -> p b n").bitcast(I32))
        for q in range(QUADRANTS):
            nc.sync.dma_start(
                out=w2_sc[32 * q : 32 * q + 4, :, :].bitcast(I32),
                in_=w2_scales[:, 4 * q : 4 * q + 4, :].rearrange("b r n -> r b n").bitcast(I32),
            )
        bias = bias_first + [bias_second[:, t : t + 1] for t in range(PACK)]
        factor = [gain_sb[:, n // PACK, n % PACK : n % PACK + 1] for n in range(2 * PACK)]

        rounded, w1_codes, w1_sc = {}, {}, {}

        def round_w1(copy, g, a, ts, tag):
            width = W1_COLUMNS[g][1] // PACK
            dst = aligned([P, len(ts), width, PACK], BF16, tag)
            src = raw[g, a].rearrange("p j (m t) -> p m j t", t=PACK)
            for i in range(0, len(ts), 2):
                copy(dst[:, i : i + 2].rearrange("p t m j -> p m j t"), src[:, :, :, ts[i] : ts[i] + 2])
            rounded[g, a, ts[0]] = dst[:].rearrange("p t m j -> p (t m j)")

        def quantize_w1(g, a, t0):
            width = W1_COLUMNS[g][1]
            if (g, a) not in w1_codes:
                w1_codes[g, a] = aligned([P, width], U32, f"w1_codes{g}_{a}")
                w1_sc[g, a] = aligned([P, width], U8, f"w1_sc{g}_{a}")
            src = rounded[g, a, t0]
            first = t0 * width // PACK
            cols = slice(first, first + src.shape[1] // PACK)
            nc.vector.quantize_mx(
                out=w1_codes[g, a][:, cols].bitcast(FP8X4), scales=w1_sc[g, a][:, cols], in_=src
            )

        def gather_words(a, first=0, n=S):
            picks = offs_sb[:, first // LIST_COLUMN : (first + n) // LIST_COLUMN]
            nc.vector.tensor_copy(v_codes[a][:, first : first + n], tab_sb[a][:].bitcast(U32).indirect(picks))

        h_ps, h_sb, planes = {}, {}, []

        def h_banks(n):
            if n == 0:
                return 0, QUARTER
            return (2 * (n + 1)) % 8, BANK

        def project(n, a, side, closing=LAST):
            first, width = h_banks(n)
            g, place = TILES[n]
            opening = (n, side) not in h_ps
            if opening:
                h_ps[n, side] = psum.tile([P, width], F32, name=f"bank{first + side}")
            cols = slice(side * width, (side + 1) * width)
            nc.tensor.matmul_mx(
                out=h_ps[n, side][:],
                lhsT=w1_codes[g, a][:, place * P : (place + 1) * P].bitcast(FP8X4),
                lhsT_scale=w1_sc[g, a][:, place * P : (place + 1) * P],
                rhs=v_codes[a][:, cols].bitcast(FP8X4),
                rhs_scale=planes[0][4 * a :, cols],
                start=opening,
                stop=(a == closing),
            )

        def project_tile(n, passes, closing=LAST):
            for a in passes:
                for side in range(S // h_banks(n)[1]):
                    project(n, a, side, closing)

        def empty_h(n, side, copy=scopy, tag=None):
            if n not in h_sb:
                h_sb[n] = aligned([P, S], F32, tag or f"h{n}")
            width = h_banks(n)[1]
            copy(h_sb[n][:, side * width : (side + 1) * width], h_ps[n, side][:])

        def empty_tile(n, tag=None):
            empty_h(n, 0, tag=tag)
            empty_h(n, 1)

        gates, picked, gated, z_codes, z_sc, acc = {}, {}, {}, {}, {}, {}

        def receivers(n, tag=None):
            if n not in picked:
                picked[n] = aligned([P, E], F32, tag or f"picked{n}")[:]
            nc.vector.tensor_copy(picked[n], h_sb[n][:].indirect(pos1_sb[:]))

        def sigmoid(n, tag=None):
            gates[n] = aligned([P, E], F32, tag)[:] if tag else picked[n]
            nc.scalar.activation(gates[n], picked[n], SIGMOID, bias=bias[n])

        def senders(n, j0, dst):
            width = dst.shape[1]
            nc.vector.tensor_tensor(
                dst,
                h_sb[n][:].indirect(pos2_sb[:, j0 // LIST_COLUMN : (j0 + width) // LIST_COLUMN]),
                gates[n][:, j0 : j0 + width],
                MULT,
            )

        def first_senders(n, tag=None):
            gated[n] = aligned([P, E], F32, tag or f"gated{n}")[:]
            senders(n, 0, gated[n])

        def weave_views(dst, tiles, run):
            return (
                dst.rearrange("p (c i t) -> p c t i", i=run, t=PACK),
                tiles.rearrange("p t (c i) -> p c t i", i=run),
            )

        def finish_on_vector(dst, tiles):
            dst, src = weave_views(dst, tiles, FINISH_RUN)
            factors = gain_sb[:, 1, :].unsqueeze(1).unsqueeze(3).to_broadcast(list(src.shape))
            nc.vector.tensor_tensor(dst, src, factors, MULT)

        def scale(n, dst, src):
            nc.scalar.activation(dst, src, COPY, scale=factor[n])

        def weave(dst, tiles):
            scopy(*weave_views(dst, tiles, RUN))

        def z_tiles(part, halves):
            tag = f"{part}_{halves[0]}"
            codes = aligned([P, len(halves) * PART], U32, f"z_codes{tag}")
            plane = aligned([P, len(halves) * PART], U8, f"z_sc{tag}")
            for i, b in enumerate(halves):
                z_codes[b, part] = codes[:, i * PART : (i + 1) * PART]
                z_sc[b, part] = plane[:, i * PART : (i + 1) * PART]
            return codes[:], plane[:]

        def quantize_z(codes, plane, woven):
            nc.vector.quantize_mx(out=codes.bitcast(FP8X4), scales=plane, in_=woven)

        def message_pass(nt, part, b, start, stop):
            nc.tensor.matmul_mx(
                out=acc[part, nt],
                lhsT=w2_sb[:, b, 2 * P * nt : 2 * P * (nt + 1)].bitcast(FP4X4),
                lhsT_scale=w2_sc[:, b, P * nt : P * (nt + 1)],
                rhs=z_codes[b, part].bitcast(FP8X4),
                rhs_scale=z_sc[b, part],
                start=start,
                stop=stop,
            )

        banks = {}

        def group_passes(part, g, b):
            if b == 0:
                banks[part, g] = psum.tile([P, GROUP, PART], F32, name=f"bank{GROUPS * (part + 1) + g}")
            for u in range(GROUP):
                acc[part, GROUP * g + u] = banks[part, g][:, u, :]
                message_pass(GROUP * g + u, part, b, b == 0 and u == 0, b == HALVES - 1 and u == GROUP - 1)

        def store(res, nt, part):
            rows = out[nt * P : (nt + res.shape[1]) * P, part * PART : (part + 1) * PART]
            nc.sync.dma_start(out=rows.rearrange("(u p) j -> p u j", p=P), in_=res)

        def leave(part, tag=None):
            res = aligned([P, GROUPS, GROUP, PART], F32, tag or f"res{part}")
            for g in range(GROUPS):
                scopy(res[:, g], banks[part, g][:])
                store(res[:, g], GROUP * g, part)

        def messages(part):
            for g in range(GROUPS):
                for b in range(HALVES):
                    group_passes(part, g, b)
            leave(part)

        def last_messages(part):
            res = [aligned([P, 1, PART], F32, f"res{part}_{nt}") for nt in range(N // P)]
            for nt in range(N // P):
                acc[part, nt] = psum.tile([P, PART], F32, name=f"bank{nt}")[:]
            for b in range(HALVES):
                for u in range(GROUP):
                    for g in range(GROUPS):
                        message_pass(GROUP * g + u, part, b, b == 0, b == HALVES - 1)
            for u in range(GROUP):
                scopy(res[u][:, 0, :], acc[part, u])
                vcopy(res[GROUP + u][:, 0, :], acc[part, GROUP + u])
                store(res[u][:], u, part)
                store(res[GROUP + u][:], GROUP + u, part)

        ALL, LOW, HIGH = (0, 1, 2, 3), (0, 1), (2, 3)
        lo, hi = slice(0, HALF_P), slice(HALF_P, P)

        def edges(tiles, part):
            return tiles[:, :, part * PART : (part + 1) * PART]

        gather_words(0)
        gather_words(1)
        round_w1(scopy, 0, 0, ALL, "rounded0_0")
        quantize_w1(0, 0, 0)
        planes.append(aligned([P, S], U8, "rounded0_0"))
        nc.vector.tensor_copy(planes[0][:], tab_sc[:].indirect(offs_sb[:]))
        project_tile(0, [0])
        project_tile(1, [0])
        gather_words(LAST)
        round_w1(scopy, 0, 1, ALL, "rounded0_1")
        quantize_w1(0, 1, 0)
        project_tile(0, [1])
        round_w1(scopy, 0, LAST, LOW, "rounded0_low")
        round_w1(scopy, 0, LAST, HIGH, "rounded0_high")
        quantize_w1(0, LAST, 0)
        project_tile(0, [LAST])
        quantize_w1(0, LAST, 2)
        for side in range(2):
            for a in (LAST, 1):
                project(1, a, side, closing=1)
        round_w1(scopy, 1, 0, ALL, "rounded1_0")
        for quarter, copy in enumerate((vcopy, vcopy, vcopy, scopy)):
            empty_h(0, quarter, copy)
        receivers(0)
        quantize_w1(1, 0, 0)
        project_tile(2, [0])
        empty_tile(1)
        receivers(1)
        project_tile(3, [0])
        round_w1(scopy, 1, 1, ALL, "rounded1_1")
        quantize_w1(1, 1, 0)
        project_tile(2, [1])
        project_tile(3, [1])
        round_w1(vcopy, 1, LAST, ALL, "rounded1_2")
        sent = aligned([P, PACK, E], F32, "sent")
        parked = aligned([P, 2, E], F32, "parked")
        sigmoid(0, "gates0")
        senders(0, 0, sent[:, 0, :])
        quantize_w1(1, LAST, 0)
        project_tile(2, [LAST])
        project_tile(3, [LAST])
        sigmoid(1, "gates1")
        senders(1, 0, sent[:, 2, :])
        nc.sync.dma_start(out=sent[lo, 1::2, :], in_=sent[hi, 0::2, :])
        round_w1(scopy, 2, 0, ALL, "rounded2_0")
        quantize_w1(2, 0, 0)
        round_w1(vcopy, 2, 1, LOW, "middle_low")
        round_w1(vcopy, 2, 1, HIGH, "middle_high")
        empty_tile(2)
        receivers(2)
        quantize_w1(2, 1, 0)
        quantize_w1(2, 1, 2)
        empty_tile(3)
        receivers(3)
        round_w1(scopy, 2, LAST, LOW, "last_low")
        round_w1(scopy, 2, LAST, HIGH, "last_high")
        quantize_w1(2, LAST, 0)
        quantize_w1(2, LAST, 2)
        for n in range(PACK, 2 * PACK):
            project_tile(n, range(PASSES))
        for n in (2, 3):
            sigmoid(n, f"gates{n}")
            senders(n, 0, parked[:, n - 2, :])
            nc.sync.dma_start(out=sent[hi, 2 * n - 4, :], in_=parked[lo, n - 2, :])
            nc.sync.dma_start(out=sent[hi, 2 * n - 3, :], in_=parked[hi, n - 2, :])
        first_z = aligned([P, PACK, E], BF16, "first_z")
        second = aligned([P, PACK, E], F32, "tab0")
        for t, tag in enumerate(("picked2", "picked3", None, None)):
            picked[PACK + t] = second[:, t, :]
            empty_tile(PACK + t, tag)
            receivers(PACK + t)
            if t == 2:
                scale(0, first_z[:, 0, :], sent[:, 0, :])
        early = aligned([P, PACK, 2 * PART], F32, "tab2")

        def gate_and_send(t):
            sigmoid(PACK + t)
            senders(PACK + t, 0, early[:, t, :])

        gate_and_send(0)
        gate_and_send(1)
        scale(1, first_z[:, 1, :], sent[:, 1, :])
        gate_and_send(2)
        scale(2, first_z[:, 2, :], sent[:, 2, :])
        gate_and_send(3)
        scale(3, first_z[:, 3, :], sent[:, 3, :])

        width = PART * PACK
        woven_10 = aligned([P, width], BF16, "woven_10")
        finish_on_vector(woven_10[:], edges(early, 0))
        woven_00 = aligned([P, width], BF16, "slot_a")
        weave(woven_00[:], edges(first_z, 0))
        quantize_z(*z_tiles(0, [0]), woven_00[:])
        for g in range(GROUPS):
            group_passes(0, g, 0)
        woven_1 = aligned([P, HALVES * width], BF16, "slot_b")
        woven_2 = aligned([P, HALVES * width], BF16, "woven_2")
        scaled = aligned([P, PACK, PART], BF16, "scaled")
        for t in range(PACK):
            scale(PACK + t, scaled[:, t, :], edges(early, 1)[:, t, :])
        weave(woven_1[:, :width], edges(first_z, 1))
        weave(woven_1[:, width:], scaled[:])
        weave(woven_2[:, :width], edges(first_z, 2))
        quantize_z(*z_tiles(0, [1]), woven_10[:])
        for g in range(GROUPS):
            group_passes(0, g, 1)
        leave(0)
        woven_03 = aligned([P, width], BF16, "woven_03")
        weave(woven_03[:], edges(first_z, 3))

        third = aligned([P, PACK, PART], F32, "tab2")
        for t in range(PACK):
            senders(PACK + t, 2 * PART, third[:, t, :])
        quantize_z(*z_tiles(1, [0, 1]), woven_1[:])
        messages(1)
        finish_on_vector(woven_2[:, width:], third[:])
        quantize_z(*z_tiles(3, [0]), woven_03[:])
        quantize_z(*z_tiles(2, [0, 1]), woven_2[:])
        messages(2)

        fourth = aligned([P, PACK, PART], F32, "slot_b")
        for t in range(PACK - 1):
            senders(PACK + t, 3 * PART, fourth[:, t, :])
        for first in (0, PIECE):
            senders(2 * PACK - 1, 3 * PART + first, fourth[:, PACK - 1, first : first + PIECE])
        codes, plane = z_tiles(3, [1])
        for first in (0, PIECE):
            cols = slice(first, first + PIECE)
            woven = aligned([P, PIECE * PACK], BF16, f"woven_13_{first}")
            finish_on_vector(woven[:], fourth[:, :, cols])
            quantize_z(codes[:, cols], plane[:, cols], woven[:])
        last_messages(PARTS - 1)
